import numpy as np
import ml_dtypes


def mxq(x, axis, fmt="e4m3"):
    dtype, down = {"e4m3": (ml_dtypes.float8_e4m3fn, 7), "e5m2": (ml_dtypes.float8_e5m2, 14)}[fmt]
    v = np.moveaxis(np.asarray(x, np.float32).astype(ml_dtypes.bfloat16).astype(np.float64), axis, -1)
    blocks = v.reshape(v.shape[:-1] + (-1, 32))
    amax = np.abs(blocks).max(-1, keepdims=True)
    byte = np.maximum(np.where(amax > 0, np.frexp(amax)[1] - 1 + 127, 0) - down, 1)
    scale = np.exp2(byte - 127.0)
    codes = (blocks / scale).astype(np.float32).astype(dtype).astype(np.float64)
    return np.moveaxis((codes * scale).reshape(v.shape), -1, axis)


WIDE = False


def mx_kscale(k):
    if not WIDE:
        return np.ones(k)
    levels = np.array([10, -10, 5, -5, 0])
    if k % 512:
        return np.exp2(np.random.permutation(np.resize(levels, k // 32))).repeat(32)
    a = np.empty((k // 512, 16))
    for p in range(k // 512):
        a[p, :8] = np.random.permutation(np.resize(levels, 8))
        for g in range(8):
            far = levels[np.abs(levels - a[p, g]) >= 10]
            a[p, g + 8] = far[np.random.randint(len(far))]
    return np.exp2(a.ravel()).repeat(32)


def f64(x):
    return np.asarray(x).astype(np.float64)


def striped(idx):
    return np.tile(np.asarray(idx).reshape(-1, 16).T, (8, 1)).astype(np.uint16)


def unstriped(offs):
    return offs[:16].T.reshape(-1).astype(np.int64)


E2M1 = np.array([0.0, 0.5, 1.0, 1.5, 2.0, 3.0, 4.0, 6.0, -0.0, -0.5, -1.0, -1.5, -2.0, -3.0, -4.0, -6.0])


def pack_weight(w, fmt):
    k, n = w.shape
    w = f64(np.asarray(w, np.float32).astype(ml_dtypes.bfloat16)).reshape(k // 32, 32, n)
    amax = np.abs(w).max(1)
    if fmt == "e4m3":
        byte = np.frexp(amax)[1] - 1 + 127 - 7
    else:
        mant, ex = np.frexp(amax / 6.0)
        byte = np.where(mant > 0.5, ex, ex - 1) + 127
    byte = np.clip(np.where(amax > 0, byte, 1), 1, 254)
    scaled = (w * np.exp2(127.0 - byte)[:, None, :]).reshape(k, n).astype(np.float32)
    by_word = np.ascontiguousarray(scaled.reshape(k // 512, 128, 4, n).transpose(0, 1, 3, 2))
    if fmt == "e4m3":
        words = by_word.astype(ml_dtypes.float8_e4m3fn).view(np.uint8)
    else:
        c = by_word.astype(ml_dtypes.float4_e2m1fn).view(np.uint8) & 0xF
        words = (c[..., 0::2] | (c[..., 1::2] << 4)).reshape(k // 512, 128, 2 * n)
    return np.ascontiguousarray(words), np.ascontiguousarray(byte.astype(np.uint8).reshape(k // 512, 16, n))


def unpack_weight(words, scales, fmt):
    g, _, n = scales.shape
    words = np.ascontiguousarray(words).reshape(g, 128, n, -1)
    if fmt == "e4m3":
        vals = words.view(ml_dtypes.float8_e4m3fn).astype(np.float64)
    else:
        nib = np.empty((g, 128, n, 4), np.uint8)
        nib[..., 0::2] = words & 0xF
        nib[..., 1::2] = words >> 4
        vals = E2M1[nib]
    vals = vals * np.repeat(np.exp2(scales.astype(np.float64) - 127.0), 8, axis=1)[..., None]
    return vals.transpose(0, 1, 3, 2).reshape(g * 512, n)


def bf(x):
    return np.asarray(x, np.float32).astype(ml_dtypes.bfloat16)


def planes(Y):
    r, m = Y.shape
    b = f64(bf(Y)).reshape(r // 32, 32, m)
    amax = np.abs(b).max(1)
    byte = np.clip(np.where(amax > 0, np.frexp(amax)[1] - 1 + 127 - 7, 1), 1, 254)
    codes = (b * np.exp2(127.0 - byte)[:, None, :]).reshape(r, m).astype(np.float32).astype(ml_dtypes.float8_e4m3fn).view(np.uint8)
    words = codes.reshape(r // 512, 128, 4, m).transpose(0, 1, 3, 2)
    return np.ascontiguousarray(words), np.ascontiguousarray(byte.astype(np.uint8).reshape(r // 512, 16, m))


D, T, I, Q, E, U, J = 512, 2048, 512, 256, 512, 1024, 512


def setup_inputs():
    n = np.random.standard_normal
    idx = np.random.permutation(T)[:I]
    idx2 = np.random.permutation(U)[:J]
    fd = mx_kscale(D)
    fi = mx_kscale(I)
    fj = mx_kscale(J)
    ti = np.ones(T)
    ti[idx] = fi
    tj = np.ones(U)
    tj[idx2] = fj
    keysp = pack_weight(n((D, T)) / fd[:, None], "e2m1")
    rkeyp = pack_weight(n((D, U)) / fd[:, None], "e4m3")
    return {
        "query": (n((D, Q)) * 0.4 / np.sqrt(D) * fd[:, None]).astype(np.float32),
        "keys_words": keysp[0],
        "keys_scales": keysp[1],
        "rkey_words": rkeyp[0],
        "rkey_scales": rkeyp[1],
        "size": (np.random.uniform(0.5, 2.0, (1, I)) * fi).astype(np.float32),
        "rsz": (np.random.uniform(0.5, 2.0, (1, J)) * fj).astype(np.float32),
        "vals": (n((E, T)) / ti).astype(np.float32),
        "rval": (n((E, U)) / tj).astype(np.float32),
        "offs": striped(idx),
        "offs2": striped(idx2),
    }


def reference(query, keys_words, keys_scales, rkey_words, rkey_scales, size, rsz, vals, rval, offs, offs2):
    idx = unstriped(offs)
    idx2 = unstriped(offs2)
    keysu = unpack_weight(keys_words, keys_scales, "e2m1")
    rkeyu = unpack_weight(rkey_words, rkey_scales, "e4m3")
    queryq = mxq(f64(query), 0, "e4m3")
    keysidxg = keysu[:, idx]
    a = queryq.T @ keysidxg
    rkeyidx2g = rkeyu[:, idx2]
    b = queryq.T @ rkeyidx2g
    m = np.maximum(np.max(a, axis=1, keepdims=True), np.max(b, axis=1, keepdims=True))
    p = np.exp(a - m)
    r = np.exp(b - m)
    z = np.sum(p, axis=1, keepdims=True) + np.sum(r, axis=1, keepdims=True)
    w = p * f64(size) / z
    x = r * f64(rsz) / z
    wt = w.T
    xt = x.T
    vt = f64(vals)[:, idx].T
    ut = f64(rval)[:, idx2].T
    vtq = mxq(vt, 0, "e4m3")
    wtq = mxq(wt, 0, "e4m3")
    utq = mxq(ut, 0, "e4m3")
    xtq = mxq(xt, 0, "e4m3")
    o = vtq.T @ wtq + utq.T @ xtq
    words, scales = planes(o)
    return o, words, scales

@@ -1,0 +1,222 @@
+from contextlib import ExitStack
+
+import concourse.mybir as mybir
+from concourse.masks import make_identity
+
+F32 = mybir.dt.float32
+BF16 = mybir.dt.bfloat16
+I32 = mybir.dt.int32
+U32 = mybir.dt.uint32
+U16 = mybir.dt.uint16
+U8 = mybir.dt.uint8
+FP8X4 = mybir.dt.float8_e4m3fn_x4
+FP4X4 = mybir.dt.float4_e2m1fn_x4
+ACT = mybir.ActivationFunctionType
+ALU = mybir.AluOpType
+AX = mybir.AxisListType
+
+P = 128
+PACK = 4
+D, T, Q, E, U, SLOTS = 512, 2048, 256, 512, 1024, 512
+HALVES = Q // P
+FLOPS = 2 * 2 * D * Q * SLOTS + 2 * 2 * SLOTS * E * Q
+ON_SCALAR = (0, 1)
+LOAD_ORDER = ((1, 0), (1, 1), (0, 0), (0, 1), (0, 2), (1, 2), (0, 3), (1, 3))
+GROUPS = (((1, 0), (1, 1), (0, 0), (0, 1)), ((0, 2), (1, 2)), ((0, 3),), ((1, 3),))
+
+
+def tile_attend_two_caches_pl_kernel(tc, query, keys_words, keys_scales, rkey_words, rkey_scales,
+                                      size, rsz, vals, rval, offs, offs2, out_0, out_1, out_2):
+    nc = tc.nc
+    with ExitStack() as ctx:
+        keep = ctx.enter_context(tc.tile_pool(name="keep", bufs=1))
+        psum = ctx.enter_context(tc.psum_pool(name="psum", bufs=1))
+
+        def sb(name, shape, dtype, reuse=None):
+            return keep.tile(shape, dtype, name=name, tag=reuse or name, align_bytes=64)
+
+        lists = [keep.tile([P, SLOTS // 16], U16, name="list0"), keep.tile([P, SLOTS // 16], U16, name="list1")]
+        key_scale_pool = [sb("ksp0", [P, T], U8), sb("ksp1", [P, U], U8)]
+        key_word_pool = [sb("kwp0", [P, T], U16), sb("kwp1", [P, U], U32)]
+
+        def load_scales(c, src):
+            rows = src[0].bitcast(I32)
+            for quad in range(4):
+                nc.sync.dma_start(out=key_scale_pool[c][32 * quad:32 * quad + 32, :].bitcast(I32),
+                                  in_=rows[4 * quad:4 * quad + 4, :].unsqueeze(0).broadcast_to([8, 4, rows.shape[1]]))
+
+        nc.sync.dma_start(lists[0][:], offs)
+        load_scales(0, keys_scales)
+        nc.sync.dma_start(out=key_word_pool[0][:].bitcast(I32), in_=keys_words[0].bitcast(I32))
+        nc.sync.dma_start(lists[1][:], offs2)
+        load_scales(1, rkey_scales)
+        q_raw = sb("q_raw", [P, PACK, Q], F32)
+        nc.sync.dma_start(out=q_raw[:], in_=query.rearrange("(p j) q -> p j q", j=PACK))
+        nc.sync.dma_start(out=key_word_pool[1][:].bitcast(I32),
+                          in_=rkey_words[0].rearrange("p n t -> p (n t)").bitcast(I32))
+        slot_w = [sb("slot_w0", [P, PACK], F32), sb("slot_w1", [P, PACK], F32)]
+        pools = (vals, rval)
+        widths = (T, U)
+        val_pool = {}
+        for c, r in LOAD_ORDER:
+            val_pool[c, r] = sb("vp%d%d" % (c, r), [P, widths[c]], F32)
+            nc.sync.dma_start(out=val_pool[c, r][:], in_=pools[c].rearrange("(m r) t -> r m t", r=PACK)[r])
+            if (c, r) == LOAD_ORDER[0]:
+                for k, src in enumerate((size, rsz)):
+                    nc.sync.dma_start(out=slot_w[k][:], in_=src.rearrange("o (p t) -> (o p) t", t=PACK))
+
+        warm = sb("warm", [P, 2], F32)
+        nc.vector.memset(warm[:, 0:1], 0.0)
+        nc.scalar.activation(out=warm[:, 1:2], in_=warm[:, 0:1], func=ACT.Exp)
+
+        ident = sb("ident", [P, P], F32)
+        make_identity(nc, ident[:])
+
+        key_scales = [sb("ks0", [P, SLOTS], U8), sb("ks1", [P, SLOTS], U8)]
+        key_words = [sb("kw0", [P, SLOTS], U16)]
+        nc.vector.tensor_copy(key_scales[0][:], key_scale_pool[0][:].indirect(lists[0][:]))
+        nc.vector.tensor_copy(key_words[0][:], key_word_pool[0][:].indirect(lists[0][:]))
+
+        q_bf = sb("q_bf", [P, Q, PACK], BF16)
+        nc.scalar.activation(out=q_bf[:].rearrange("p (c i) t -> p c t i", i=4),
+                             in_=q_raw[:].rearrange("p t (c i) -> p c t i", i=4), func=ACT.Copy)
+        nc.vector.tensor_copy(key_scales[1][:], key_scale_pool[1][:].indirect(lists[1][:]))
+        q_codes = sb("q_codes", [P, Q], U32)
+        q_scales = sb("q_scales", [P, Q], U8)
+        nc.vector.quantize_mx(out=q_codes[:].bitcast(FP8X4), scales=q_scales[:],
+                              in_=q_bf[:].rearrange("p q t -> p (q t)"))
+        key_words.append(sb("kw1", [P, SLOTS], U32, reuse="q_bf"))
+        nc.vector.tensor_copy(key_words[1][:], key_word_pool[1][:].indirect(lists[1][:]))
+
+        spread = []
+        for c in range(2):
+            bank = psum.tile([P, PACK, P], F32, name="spread%d" % c)
+            for t in range(PACK):
+                nc.tensor.transpose(bank[:, t, :], slot_w[c][:, t:t + 1].to_broadcast([P, P]), ident[:])
+            spread.append(bank)
+
+        fmts = (FP4X4, FP8X4)
+        scores = {}
+        for c in range(2):
+            for h in range(HALVES):
+                scores[c, h] = psum.tile([P, SLOTS], F32, name="score%d%d" % (c, h), tag="big%d%d" % (c, h))
+                nc.tensor.matmul_mx(out=scores[c, h][:],
+                                    lhsT=q_codes[:, h * P:(h + 1) * P].bitcast(FP8X4),
+                                    lhsT_scale=q_scales[:, h * P:(h + 1) * P],
+                                    rhs=key_words[c][:].bitcast(fmts[c]), rhs_scale=key_scales[c][:],
+                                    start=True, stop=True)
+
+        def turn(src_bf, bank):
+            words = src_bf.bitcast(F32)
+            for u in range(2):
+                nc.tensor.transpose(bank[:, u, :], words[:, u::2], ident[:])
+
+        v_codes, v_scales = {}, {}
+        v_grouped = [sb("vg%d" % g, [P, len(group), P, 2], F32) for g, group in enumerate(GROUPS)]
+        place = {cr: (g, k) for g, group in enumerate(GROUPS) for k, cr in enumerate(group)}
+
+        def values(c, r, reuse=None):
+            picked = sb("picked%d%d" % (c, r), [P, SLOTS], BF16)
+            if c == 1 and r in ON_SCALAR:
+                cast = sb("cast%d" % r, [P, widths[c]], BF16, reuse=reuse)
+                nc.scalar.activation(out=cast[:], in_=val_pool[c, r][:], func=ACT.Copy)
+                nc.scalar.activation(out=picked[:], in_=cast[:].indirect(lists[c][:]), func=ACT.Copy)
+            else:
+                nc.vector.tensor_copy(picked[:], val_pool[c, r][:].indirect(lists[c][:]))
+            bank = psum.tile([P, 2, P], F32, name="vturn", tag="turn", bufs=2)
+            turn(picked[:], bank)
+            g, k = place[c, r]
+            nc.scalar.copy(out=v_grouped[g][:, k], in_=bank[:].rearrange("p u m -> p m u"))
+
+        def quantize_values(g, reuse=None):
+            n = len(GROUPS[g])
+            codes = sb("vc%d" % g, [P, n * P], U32, reuse=reuse)
+            scales = sb("vs%d" % g, [P, n * P], U8)
+            nc.vector.quantize_mx(out=codes[:].bitcast(FP8X4), scales=scales[:],
+                                  in_=v_grouped[g][:].rearrange("p k m u -> p (k m u)").bitcast(BF16))
+            for k, cr in enumerate(GROUPS[g]):
+                v_codes[cr] = codes[:, k * P:(k + 1) * P]
+                v_scales[cr] = scales[:, k * P:(k + 1) * P]
+
+        values(1, 0)
+
+        row_max = sb("row_max", [P, HALVES, 2], F32)
+        neg_max = sb("neg_max", [P, HALVES], F32)
+        part_sum = sb("part_sum", [P, HALVES, 2], F32)
+        probs = {}
+        for h in range(HALVES):
+            nc.vector.tensor_reduce(out=row_max[:, h, 0:1], in_=scores[0, h][:], axis=AX.X, op=ALU.max)
+        for h in range(HALVES):
+            nc.vector.tensor_reduce(out=row_max[:, h, 1:2], in_=scores[1, h][:], axis=AX.X, op=ALU.max)
+            nc.vector.tensor_reduce(out=neg_max[:, h:h + 1], in_=row_max[:, h, :], axis=AX.X, op=ALU.max, negate=True)
+            for c in range(2):
+                probs[c, h] = sb("probs%d%d" % (c, h), [P, SLOTS], F32)
+                nc.scalar.activation(out=probs[c, h][:], in_=scores[c, h][:], func=ACT.Exp,
+                                     bias=neg_max[:, h:h + 1], scale=1.0, accum_out=part_sum[:, h, c:c + 1])
+        values(0, 0)
+        values(1, 1, reuse="neg_max")
+        row_sum = sb("row_sum", [P, HALVES], F32, reuse="vp00")
+        inv_sum = sb("inv_sum", [P, HALVES], F32)
+
+        w_grouped = []
+        for h in range(HALVES):
+            nc.vector.tensor_tensor(out=row_sum[:, h:h + 1], in0=part_sum[:, h, 0:1], in1=part_sum[:, h, 1:2], op=ALU.add)
+            nc.vector.reciprocal(out=inv_sum[:, h:h + 1], in_=row_sum[:, h:h + 1])
+            bank = psum.tile([P, 2, 2, P], F32, name="wturn%d" % h, tag="big1%d" % h)
+            for c in range(2):
+                weights = sb("weights%d%d" % (c, h), [P, SLOTS], BF16)
+                nc.vector.scalar_tensor_tensor(
+                    out=weights[:].rearrange("p (s t) -> p s t", t=PACK),
+                    in0=probs[c, h][:].rearrange("p (s t) -> p s t", t=PACK),
+                    scalar=inv_sum[:, h:h + 1], in1=spread[c][:].rearrange("p t s -> p s t"),
+                    op0=ALU.mult, op1=ALU.mult)
+                turn(weights[:], bank[:, c])
+            w_grouped.append(sb("wg%d" % h, [P, 2, P, 2], F32))
+            nc.scalar.copy(out=w_grouped[h][:], in_=bank[:].rearrange("p c u q -> p c q u"))
+        values(0, 1)
+        values(0, 2)
+        values(1, 2)
+        w_codes = sb("wc", [P, HALVES, 2 * P], U32, reuse="vp12")
+        w_scales = sb("ws", [P, HALVES, 2 * P], U8)
+        for h in range(HALVES):
+            nc.vector.quantize_mx(out=w_codes[:, h, :].bitcast(FP8X4), scales=w_scales[:, h, :],
+                                  in_=w_grouped[h][:].rearrange("p c q u -> p (c q u)").bitcast(BF16))
+        quantize_values(0, reuse="vp02")
+        values(0, 3)
+        quantize_values(1, reuse="vp03")
+        values(1, 3)
+        quantize_values(2, reuse="vp13")
+        quantize_values(3)
+
+        result = [psum.tile([P, PACK, P], F32, name="result%d" % h, tag="big0%d" % h) for h in range(HALVES)]
+        out_sb = [sb("out_first", [P, PACK - 1, Q], F32), sb("out_last", [P, 1, Q], F32)]
+        out_rows = out_0.rearrange("(p r) q -> p r q", r=PACK)
+        for r in range(PACK):
+            for c in range(2):
+                for h in range(HALVES):
+                    nc.tensor.matmul_mx(out=result[h][:, r, :],
+                                        lhsT=v_codes[c, r].bitcast(FP8X4), lhsT_scale=v_scales[c, r],
+                                        rhs=w_codes[:, h, c * P:(c + 1) * P].bitcast(FP8X4),
+                                        rhs_scale=w_scales[:, h, c * P:(c + 1) * P],
+                                        start=(c == 0), stop=(c == 1))
+            if r == PACK - 2:
+                for h in range(HALVES):
+                    nc.scalar.copy(out=out_sb[0][:, :, h * P:(h + 1) * P], in_=result[h][:, 0:PACK - 1, :])
+                nc.sync.dma_start(out=out_rows[:, 0:PACK - 1, :], in_=out_sb[0][:])
+
+        o_codes = sb("o_codes", [P, Q], U32)
+        o_scales = sb("o_scales", [P, Q], U8)
+        o_bf = [sb("o_bf%d" % h, [P, P, PACK], BF16) for h in range(HALVES)]
+        nc.vector.tensor_copy(out=o_bf[0][:], in_=result[0][:].rearrange("p r q -> p q r"))
+        nc.scalar.copy(out=o_bf[1][:], in_=result[1][:].rearrange("p r q -> p q r"))
+        for h in range(HALVES):
+            nc.vector.quantize_mx(out=o_codes[:, h * P:(h + 1) * P].bitcast(FP8X4), scales=o_scales[:, h * P:(h + 1) * P],
+                                  in_=o_bf[h][:].rearrange("p q r -> p (q r)"))
+        for h in (1, 0):
+            nc.scalar.copy(out=out_sb[1][:, 0, h * P:(h + 1) * P], in_=result[h][:, PACK - 1, :])
+        nc.scalar.dma_start(out=out_rows[:, PACK - 1:PACK, :], in_=out_sb[1][:])
+        nc.sync.dma_start(out=out_1[0].rearrange("p c t -> p (c t)").bitcast(I32), in_=o_codes[:].bitcast(I32))
+        for quad in range(4):
+            queue = nc.sync if quad < 2 else nc.scalar
+            queue.dma_start(out=out_2[0, 4 * quad:4 * quad + 4, :].bitcast(I32),
+                            in_=o_scales[32 * quad:32 * quad + 4, :].bitcast(I32))

@@ -20,9 +20,8 @@ PACK = 4
 D, T, Q, E, U, SLOTS = 512, 2048, 256, 512, 1024, 512
 HALVES = Q // P
 FLOPS = 2 * 2 * D * Q * SLOTS + 2 * 2 * SLOTS * E * Q
-ON_SCALAR = (0, 1)
-LOAD_ORDER = ((1, 0), (1, 1), (0, 0), (0, 1), (0, 2), (1, 2), (0, 3), (1, 3))
-GROUPS = (((1, 0), (1, 1), (0, 0), (0, 1)), ((0, 2), (1, 2)), ((0, 3),), ((1, 3),))
+LOAD_ORDER = ((1, 0), (1, 1), (0, 0), (1, 2), (0, 1), (0, 2), (0, 3), (1, 3))
+GROUPS = (((1, 0), (0, 0)), ((1, 1), (0, 1)), ((0, 2), (1, 2)), ((0, 3),), ((1, 3),))
 
 
 def tile_attend_two_caches_pl_kernel(tc, query, keys_words, keys_scales, rkey_words, rkey_scales,
@@ -49,9 +48,9 @@ def tile_attend_two_caches_pl_kernel(tc, query, keys_words, keys_scales, rkey_wo
         load_scales(0, keys_scales)
         nc.sync.dma_start(out=key_word_pool[0][:].bitcast(I32), in_=keys_words[0].bitcast(I32))
         nc.sync.dma_start(lists[1][:], offs2)
-        load_scales(1, rkey_scales)
         q_raw = sb("q_raw", [P, PACK, Q], F32)
         nc.sync.dma_start(out=q_raw[:], in_=query.rearrange("(p j) q -> p j q", j=PACK))
+        load_scales(1, rkey_scales)
         nc.sync.dma_start(out=key_word_pool[1][:].bitcast(I32),
                           in_=rkey_words[0].rearrange("p n t -> p (n t)").bitcast(I32))
         slot_w = [sb("slot_w0", [P, PACK], F32), sb("slot_w1", [P, PACK], F32)]
@@ -88,13 +87,6 @@ def tile_attend_two_caches_pl_kernel(tc, query, keys_words, keys_scales, rkey_wo
         key_words.append(sb("kw1", [P, SLOTS], U32, reuse="q_bf"))
         nc.vector.tensor_copy(key_words[1][:], key_word_pool[1][:].indirect(lists[1][:]))
 
-        spread = []
-        for c in range(2):
-            bank = psum.tile([P, PACK, P], F32, name="spread%d" % c)
-            for t in range(PACK):
-                nc.tensor.transpose(bank[:, t, :], slot_w[c][:, t:t + 1].to_broadcast([P, P]), ident[:])
-            spread.append(bank)
-
         fmts = (FP4X4, FP8X4)
         scores = {}
         for c in range(2):
@@ -106,90 +98,112 @@ def tile_attend_two_caches_pl_kernel(tc, query, keys_words, keys_scales, rkey_wo
                                     rhs=key_words[c][:].bitcast(fmts[c]), rhs_scale=key_scales[c][:],
                                     start=True, stop=True)
 
+        spread = []
+        for c in range(2):
+            bank = psum.tile([P, SLOTS], F32, name="spread%d" % c)
+            for t in range(PACK):
+                nc.tensor.transpose(bank[:, t::PACK], slot_w[c][:, t:t + 1].to_broadcast([P, P]), ident[:])
+            spread.append(bank)
+
         def turn(src_bf, bank):
             words = src_bf.bitcast(F32)
             for u in range(2):
                 nc.tensor.transpose(bank[:, u, :], words[:, u::2], ident[:])
 
         v_codes, v_scales = {}, {}
-        v_grouped = [sb("vg%d" % g, [P, len(group), P, 2], F32) for g, group in enumerate(GROUPS)]
+        early = sb("vg_early", [P, 4, P, 2], F32)
+        v_grouped = [early[:, 0:2], early[:, 2:4]] + [sb("vg%d" % g, [P, len(GROUPS[g]), P, 2], F32)[:] for g in (2, 3, 4)]
         place = {cr: (g, k) for g, group in enumerate(GROUPS) for k, cr in enumerate(group)}
+        banks, casts = {}, {}
+
+        def cast(engine, r, reuse=None):
+            casts[r] = sb("cast%d" % r, [P, U], BF16, reuse=reuse)
+            if engine == "scalar":
+                nc.scalar.activation(out=casts[r][:], in_=val_pool[1, r][:], func=ACT.Copy)
+            else:
+                nc.vector.tensor_copy(out=casts[r][:], in_=val_pool[1, r][:])
 
         def values(c, r, reuse=None):
-            picked = sb("picked%d%d" % (c, r), [P, SLOTS], BF16)
-            if c == 1 and r in ON_SCALAR:
-                cast = sb("cast%d" % r, [P, widths[c]], BF16, reuse=reuse)
-                nc.scalar.activation(out=cast[:], in_=val_pool[c, r][:], func=ACT.Copy)
-                nc.scalar.activation(out=picked[:], in_=cast[:].indirect(lists[c][:]), func=ACT.Copy)
+            picked = sb("picked%d%d" % (c, r), [P, SLOTS], BF16, reuse=reuse)
+            if c == 1 and r in casts:
+                nc.scalar.activation(out=picked[:], in_=casts[r][:].indirect(lists[c][:]), func=ACT.Copy)
             else:
                 nc.vector.tensor_copy(picked[:], val_pool[c, r][:].indirect(lists[c][:]))
-            bank = psum.tile([P, 2, P], F32, name="vturn", tag="turn", bufs=2)
-            turn(picked[:], bank)
             g, k = place[c, r]
-            nc.scalar.copy(out=v_grouped[g][:, k], in_=bank[:].rearrange("p u m -> p m u"))
+            if g not in banks:
+                banks[g] = psum.tile([P, 2, 2, P], F32, name="vturn%d" % g, tag="turn", bufs=2)
+            turn(picked[:], banks[g][:, k])
 
-        def quantize_values(g, reuse=None):
+        def copy_out(g):
             n = len(GROUPS[g])
-            codes = sb("vc%d" % g, [P, n * P], U32, reuse=reuse)
-            scales = sb("vs%d" % g, [P, n * P], U8)
-            nc.vector.quantize_mx(out=codes[:].bitcast(FP8X4), scales=scales[:],
-                                  in_=v_grouped[g][:].rearrange("p k m u -> p (k m u)").bitcast(BF16))
-            for k, cr in enumerate(GROUPS[g]):
+            nc.scalar.copy(out=v_grouped[g], in_=banks[g][:, 0:n].rearrange("p k u m -> p k m u"))
+
+        def quantize_values(src, members, codes, scales):
+            nc.vector.quantize_mx(out=codes.bitcast(FP8X4), scales=scales,
+                                  in_=src.rearrange("p k m u -> p (k m u)").bitcast(BF16))
+            for k, cr in enumerate(members):
                 v_codes[cr] = codes[:, k * P:(k + 1) * P]
                 v_scales[cr] = scales[:, k * P:(k + 1) * P]
 
+        cast("scalar", 0)
         values(1, 0)
 
-        row_max = sb("row_max", [P, HALVES, 2], F32)
+        neg_first = sb("neg_first", [P, HALVES], F32)
         neg_max = sb("neg_max", [P, HALVES], F32)
-        part_sum = sb("part_sum", [P, HALVES, 2], F32)
-        probs = {}
+        row_sum = sb("row_sum", [P, HALVES], F32)
+        neg_scores = [sb("neg_scores%d" % h, [P, 2, SLOTS], F32) for h in range(HALVES)]
+        probs = [sb("probs%d" % h, [P, 2, SLOTS], F32) for h in range(HALVES)]
         for h in range(HALVES):
-            nc.vector.tensor_reduce(out=row_max[:, h, 0:1], in_=scores[0, h][:], axis=AX.X, op=ALU.max)
+            nc.vector.tensor_scalar(out=neg_scores[h][:, 0, :], in0=scores[0, h][:], scalar1=-1.0, scalar2=None,
+                                    op0=ALU.mult, op1=ALU.min, accum_out=neg_first[:, h:h + 1])
         for h in range(HALVES):
-            nc.vector.tensor_reduce(out=row_max[:, h, 1:2], in_=scores[1, h][:], axis=AX.X, op=ALU.max)
-            nc.vector.tensor_reduce(out=neg_max[:, h:h + 1], in_=row_max[:, h, :], axis=AX.X, op=ALU.max, negate=True)
-            for c in range(2):
-                probs[c, h] = sb("probs%d%d" % (c, h), [P, SLOTS], F32)
-                nc.scalar.activation(out=probs[c, h][:], in_=scores[c, h][:], func=ACT.Exp,
-                                     bias=neg_max[:, h:h + 1], scale=1.0, accum_out=part_sum[:, h, c:c + 1])
+            nc.vector.tensor_scalar(out=neg_scores[h][:, 1, :], in0=scores[1, h][:], scalar1=-1.0,
+                                    scalar2=neg_first[:, h:h + 1], op0=ALU.mult, op1=ALU.min,
+                                    accum_out=neg_max[:, h:h + 1])
+            nc.scalar.activation(out=probs[h][:], in_=neg_scores[h][:], func=ACT.Exp,
+                                 bias=neg_max[:, h:h + 1], scale=-1.0, accum_out=row_sum[:, h:h + 1])
         values(0, 0)
-        values(1, 1, reuse="neg_max")
-        row_sum = sb("row_sum", [P, HALVES], F32, reuse="vp00")
-        inv_sum = sb("inv_sum", [P, HALVES], F32)
+        cast("scalar", 1, reuse="neg_scores1")
+        values(1, 1)
+        copy_out(0)
 
         w_grouped = []
         for h in range(HALVES):
-            nc.vector.tensor_tensor(out=row_sum[:, h:h + 1], in0=part_sum[:, h, 0:1], in1=part_sum[:, h, 1:2], op=ALU.add)
-            nc.vector.reciprocal(out=inv_sum[:, h:h + 1], in_=row_sum[:, h:h + 1])
+            inv_sum = sb("inv_sum%d" % h, [P, 1], F32, reuse="vp00")
+            nc.vector.reciprocal(out=inv_sum[:], in_=row_sum[:, h:h + 1])
             bank = psum.tile([P, 2, 2, P], F32, name="wturn%d" % h, tag="big1%d" % h)
             for c in range(2):
                 weights = sb("weights%d%d" % (c, h), [P, SLOTS], BF16)
-                nc.vector.scalar_tensor_tensor(
-                    out=weights[:].rearrange("p (s t) -> p s t", t=PACK),
-                    in0=probs[c, h][:].rearrange("p (s t) -> p s t", t=PACK),
-                    scalar=inv_sum[:, h:h + 1], in1=spread[c][:].rearrange("p t s -> p s t"),
-                    op0=ALU.mult, op1=ALU.mult)
+                nc.vector.scalar_tensor_tensor(out=weights[:], in0=probs[h][:, c, :], scalar=inv_sum[:],
+                                               in1=spread[c][:], op0=ALU.mult, op1=ALU.mult)
                 turn(weights[:], bank[:, c])
             w_grouped.append(sb("wg%d" % h, [P, 2, P, 2], F32))
             nc.scalar.copy(out=w_grouped[h][:], in_=bank[:].rearrange("p c u q -> p c q u"))
-        values(0, 1)
+        cast("vector", 2)
+        values(0, 1, reuse="probs1")
+        copy_out(1)
+        values(1, 2, reuse="probs1")
         values(0, 2)
-        values(1, 2)
-        w_codes = sb("wc", [P, HALVES, 2 * P], U32, reuse="vp12")
+        copy_out(2)
+        mid_codes = sb("mid_codes", [P, 2, 4 * P], U32, reuse="vp02")
+        w_codes = mid_codes[:, 0, :].rearrange("p (h n) -> p h n", h=HALVES)
         w_scales = sb("ws", [P, HALVES, 2 * P], U8)
         for h in range(HALVES):
             nc.vector.quantize_mx(out=w_codes[:, h, :].bitcast(FP8X4), scales=w_scales[:, h, :],
                                   in_=w_grouped[h][:].rearrange("p c q u -> p (c q u)").bitcast(BF16))
-        quantize_values(0, reuse="vp02")
+        scales = sb("vs", [P, 8 * P], U8)
+        quantize_values(early[:], GROUPS[0] + GROUPS[1], mid_codes[:, 1, :], scales[:, 0:4 * P])
         values(0, 3)
-        quantize_values(1, reuse="vp03")
+        copy_out(3)
         values(1, 3)
-        quantize_values(2, reuse="vp13")
-        quantize_values(3)
+        copy_out(4)
+        codes = sb("vc_late", [P, 4 * P], U32, reuse="vp13")
+        quantize_values(v_grouped[2], GROUPS[2], codes[:, 0:2 * P], scales[:, 4 * P:6 * P])
+        quantize_values(v_grouped[3], GROUPS[3], codes[:, 2 * P:3 * P], scales[:, 6 * P:7 * P])
+        quantize_values(v_grouped[4], GROUPS[4], codes[:, 3 * P:4 * P], scales[:, 7 * P:8 * P])
 
         result = [psum.tile([P, PACK, P], F32, name="result%d" % h, tag="big0%d" % h) for h in range(HALVES)]
-        out_sb = [sb("out_first", [P, PACK - 1, Q], F32), sb("out_last", [P, 1, Q], F32)]
+        out_sb = [sb("out_first", [P, 2, Q], F32), sb("out_last", [P, 2, Q], F32)]
         out_rows = out_0.rearrange("(p r) q -> p r q", r=PACK)
         for r in range(PACK):
             for c in range(2):
@@ -199,23 +213,23 @@ def tile_attend_two_caches_pl_kernel(tc, query, keys_words, keys_scales, rkey_wo
                                         rhs=w_codes[:, h, c * P:(c + 1) * P].bitcast(FP8X4),
                                         rhs_scale=w_scales[:, h, c * P:(c + 1) * P],
                                         start=(c == 0), stop=(c == 1))
-            if r == PACK - 2:
+            if r == 1:
                 for h in range(HALVES):
-                    nc.scalar.copy(out=out_sb[0][:, :, h * P:(h + 1) * P], in_=result[h][:, 0:PACK - 1, :])
-                nc.sync.dma_start(out=out_rows[:, 0:PACK - 1, :], in_=out_sb[0][:])
+                    nc.scalar.copy(out=out_sb[0][:, :, h * P:(h + 1) * P], in_=result[h][:, 0:2, :])
+                nc.sync.dma_start(out=out_rows[:, 0:2, :], in_=out_sb[0][:])
 
         o_codes = sb("o_codes", [P, Q], U32)
         o_scales = sb("o_scales", [P, Q], U8)
         o_bf = [sb("o_bf%d" % h, [P, P, PACK], BF16) for h in range(HALVES)]
         nc.vector.tensor_copy(out=o_bf[0][:], in_=result[0][:].rearrange("p r q -> p q r"))
         nc.scalar.copy(out=o_bf[1][:], in_=result[1][:].rearrange("p r q -> p q r"))
+        nc.vector.tensor_copy(out=out_sb[1][:, :, 0:P], in_=result[0][:, 2:4, :])
+        nc.scalar.copy(out=out_sb[1][:, :, P:Q], in_=result[1][:, 2:4, :])
+        nc.sync.dma_start(out=out_rows[:, 2:4, :], in_=out_sb[1][:])
         for h in range(HALVES):
             nc.vector.quantize_mx(out=o_codes[:, h * P:(h + 1) * P].bitcast(FP8X4), scales=o_scales[:, h * P:(h + 1) * P],
                                   in_=o_bf[h][:].rearrange("p q r -> p (q r)"))
-        for h in (1, 0):
-            nc.scalar.copy(out=out_sb[1][:, 0, h * P:(h + 1) * P], in_=result[h][:, PACK - 1, :])
-        nc.scalar.dma_start(out=out_rows[:, PACK - 1:PACK, :], in_=out_sb[1][:])
-        nc.sync.dma_start(out=out_1[0].rearrange("p c t -> p (c t)").bitcast(I32), in_=o_codes[:].bitcast(I32))
+        nc.scalar.dma_start(out=out_1[0].rearrange("p c t -> p (c t)").bitcast(I32), in_=o_codes[:].bitcast(I32))
         for quad in range(4):
             queue = nc.sync if quad < 2 else nc.scalar
             queue.dma_start(out=out_2[0, 4 * quad:4 * quad + 4, :].bitcast(I32),

@@ -13,15 +13,16 @@ FP8X4 = mybir.dt.float8_e4m3fn_x4
 FP4X4 = mybir.dt.float4_e2m1fn_x4
 ACT = mybir.ActivationFunctionType
 ALU = mybir.AluOpType
-AX = mybir.AxisListType
 
 P = 128
 PACK = 4
+QUADRANTS = 4
 D, T, Q, E, U, SLOTS = 512, 2048, 256, 512, 1024, 512
 HALVES = Q // P
 FLOPS = 2 * 2 * D * Q * SLOTS + 2 * 2 * SLOTS * E * Q
 LOAD_ORDER = ((1, 0), (1, 1), (0, 0), (1, 2), (0, 1), (0, 2), (0, 3), (1, 3))
 GROUPS = (((1, 0), (0, 0)), ((1, 1), (0, 1)), ((0, 2), (1, 2)), ((0, 3),), ((1, 3),))
+TURN_BANKS = 4
 
 
 def tile_attend_two_caches_pl_kernel(tc, query, keys_words, keys_scales, rkey_words, rkey_scales,
@@ -38,56 +39,55 @@ def tile_attend_two_caches_pl_kernel(tc, query, keys_words, keys_scales, rkey_wo
         key_scale_pool = [sb("ksp0", [P, T], U8), sb("ksp1", [P, U], U8)]
         key_word_pool = [sb("kwp0", [P, T], U16), sb("kwp1", [P, U], U32)]
 
+        nc.vector.memset(key_scale_pool[0][:].bitcast(I32), 0)
+        warm = sb("warm", [P, 2], F32)
+        nc.vector.memset(warm[:, 0:1], 0.0)
+        nc.vector.memset(key_scale_pool[1][:].bitcast(I32), 0)
+
         def load_scales(c, src):
-            rows = src[0].bitcast(I32)
-            for quad in range(4):
-                nc.sync.dma_start(out=key_scale_pool[c][32 * quad:32 * quad + 32, :].bitcast(I32),
-                                  in_=rows[4 * quad:4 * quad + 4, :].unsqueeze(0).broadcast_to([8, 4, rows.shape[1]]))
+            for quad in range(QUADRANTS):
+                nc.scalar.dma_start(out=key_scale_pool[c][32 * quad:32 * quad + 4, :].bitcast(I32),
+                                    in_=src[0, 4 * quad:4 * quad + 4, :].bitcast(I32))
 
         nc.sync.dma_start(lists[0][:], offs)
-        load_scales(0, keys_scales)
         nc.sync.dma_start(out=key_word_pool[0][:].bitcast(I32), in_=keys_words[0].bitcast(I32))
+        load_scales(0, keys_scales)
+        nc.scalar.activation(out=warm[:, 1:2], in_=warm[:, 0:1], func=ACT.Exp)
         nc.sync.dma_start(lists[1][:], offs2)
+        nc.sync.dma_start(out=key_word_pool[1][:].bitcast(I32),
+                          in_=rkey_words[0].rearrange("p n t -> p (n t)").bitcast(I32))
         q_raw = sb("q_raw", [P, PACK, Q], F32)
         nc.sync.dma_start(out=q_raw[:], in_=query.rearrange("(p j) q -> p j q", j=PACK))
         load_scales(1, rkey_scales)
-        nc.sync.dma_start(out=key_word_pool[1][:].bitcast(I32),
-                          in_=rkey_words[0].rearrange("p n t -> p (n t)").bitcast(I32))
         slot_w = [sb("slot_w0", [P, PACK], F32), sb("slot_w1", [P, PACK], F32)]
+        for c, src in enumerate((size, rsz)):
+            nc.sync.dma_start(out=slot_w[c][:], in_=src.rearrange("o (p t) -> (o p) t", t=PACK))
         pools = (vals, rval)
         widths = (T, U)
         val_pool = {}
         for c, r in LOAD_ORDER:
             val_pool[c, r] = sb("vp%d%d" % (c, r), [P, widths[c]], F32)
             nc.sync.dma_start(out=val_pool[c, r][:], in_=pools[c].rearrange("(m r) t -> r m t", r=PACK)[r])
-            if (c, r) == LOAD_ORDER[0]:
-                for k, src in enumerate((size, rsz)):
-                    nc.sync.dma_start(out=slot_w[k][:], in_=src.rearrange("o (p t) -> (o p) t", t=PACK))
-
-        warm = sb("warm", [P, 2], F32)
-        nc.vector.memset(warm[:, 0:1], 0.0)
-        nc.scalar.activation(out=warm[:, 1:2], in_=warm[:, 0:1], func=ACT.Exp)
 
         ident = sb("ident", [P, P], F32)
         make_identity(nc, ident[:])
 
-        key_scales = [sb("ks0", [P, SLOTS], U8), sb("ks1", [P, SLOTS], U8)]
-        key_words = [sb("kw0", [P, SLOTS], U16)]
+        key_scales = [sb("ks0", [P, SLOTS], U8)]
+        key_words = [sb("kw0", [P, SLOTS], U16), sb("kw1", [P, SLOTS], U32)]
+        for c in range(2):
+            nc.vector.tensor_copy(key_words[c][:], key_word_pool[c][:].indirect(lists[c][:]))
         nc.vector.tensor_copy(key_scales[0][:], key_scale_pool[0][:].indirect(lists[0][:]))
-        nc.vector.tensor_copy(key_words[0][:], key_word_pool[0][:].indirect(lists[0][:]))
-
         q_bf = sb("q_bf", [P, Q, PACK], BF16)
         nc.scalar.activation(out=q_bf[:].rearrange("p (c i) t -> p c t i", i=4),
                              in_=q_raw[:].rearrange("p t (c i) -> p c t i", i=4), func=ACT.Copy)
-        nc.vector.tensor_copy(key_scales[1][:], key_scale_pool[1][:].indirect(lists[1][:]))
-        q_codes = sb("q_codes", [P, Q], U32)
+        q_codes = sb("q_codes", [P, Q], U32, reuse="ksp0")
         q_scales = sb("q_scales", [P, Q], U8)
         nc.vector.quantize_mx(out=q_codes[:].bitcast(FP8X4), scales=q_scales[:],
                               in_=q_bf[:].rearrange("p q t -> p (q t)"))
-        key_words.append(sb("kw1", [P, SLOTS], U32, reuse="q_bf"))
-        nc.vector.tensor_copy(key_words[1][:], key_word_pool[1][:].indirect(lists[1][:]))
+        key_scales.append(sb("ks1", [P, SLOTS], U8, reuse="q_bf"))
+        nc.vector.tensor_copy(key_scales[1][:], key_scale_pool[1][:].indirect(lists[1][:]))
 
-        fmts = (FP4X4, FP8X4)
+        key_formats = (FP4X4, FP8X4)
         scores = {}
         for c in range(2):
             for h in range(HALVES):
@@ -95,15 +95,8 @@ def tile_attend_two_caches_pl_kernel(tc, query, keys_words, keys_scales, rkey_wo
                 nc.tensor.matmul_mx(out=scores[c, h][:],
                                     lhsT=q_codes[:, h * P:(h + 1) * P].bitcast(FP8X4),
                                     lhsT_scale=q_scales[:, h * P:(h + 1) * P],
-                                    rhs=key_words[c][:].bitcast(fmts[c]), rhs_scale=key_scales[c][:],
+                                    rhs=key_words[c][:].bitcast(key_formats[c]), rhs_scale=key_scales[c][:],
                                     start=True, stop=True)
-
-        spread = []
-        for c in range(2):
-            bank = psum.tile([P, SLOTS], F32, name="spread%d" % c)
-            for t in range(PACK):
-                nc.tensor.transpose(bank[:, t::PACK], slot_w[c][:, t:t + 1].to_broadcast([P, P]), ident[:])
-            spread.append(bank)
 
         def turn(src_bf, bank):
             words = src_bf.bitcast(F32)
@@ -116,22 +109,28 @@ def tile_attend_two_caches_pl_kernel(tc, query, keys_words, keys_scales, rkey_wo
         place = {cr: (g, k) for g, group in enumerate(GROUPS) for k, cr in enumerate(group)}
         banks, casts = {}, {}
 
-        def cast(engine, r, reuse=None):
+        def cast(r, reuse=None):
             casts[r] = sb("cast%d" % r, [P, U], BF16, reuse=reuse)
-            if engine == "scalar":
-                nc.scalar.activation(out=casts[r][:], in_=val_pool[1, r][:], func=ACT.Copy)
-            else:
-                nc.vector.tensor_copy(out=casts[r][:], in_=val_pool[1, r][:])
+            nc.scalar.activation(out=casts[r][:], in_=val_pool[1, r][:], func=ACT.Copy)
 
         def values(c, r, reuse=None):
+            turn_values(c, r, pick(c, r, reuse))
+
+        def pick(c, r, reuse=None):
             picked = sb("picked%d%d" % (c, r), [P, SLOTS], BF16, reuse=reuse)
             if c == 1 and r in casts:
                 nc.scalar.activation(out=picked[:], in_=casts[r][:].indirect(lists[c][:]), func=ACT.Copy)
             else:
                 nc.vector.tensor_copy(picked[:], val_pool[c, r][:].indirect(lists[c][:]))
+            return picked
+
+        def turn_values(c, r, picked):
             g, k = place[c, r]
             if g not in banks:
-                banks[g] = psum.tile([P, 2, 2, P], F32, name="vturn%d" % g, tag="turn", bufs=2)
+                if g < HALVES:
+                    banks[g] = psum.tile([P, 2, 2, P], F32, name="vturn%d" % g, tag="big1%d" % g)
+                else:
+                    banks[g] = psum.tile([P, 2, 2, P], F32, name="vturn%d" % g, tag="turn", bufs=TURN_BANKS)
             turn(picked[:], banks[g][:, k])
 
         def copy_out(g):
@@ -145,33 +144,43 @@ def tile_attend_two_caches_pl_kernel(tc, query, keys_words, keys_scales, rkey_wo
                 v_codes[cr] = codes[:, k * P:(k + 1) * P]
                 v_scales[cr] = scales[:, k * P:(k + 1) * P]
 
-        cast("scalar", 0)
-        values(1, 0)
+        cast(0)
+        first_picked = pick(1, 0)
+        cast(1)
 
         neg_first = sb("neg_first", [P, HALVES], F32)
         neg_max = sb("neg_max", [P, HALVES], F32)
         row_sum = sb("row_sum", [P, HALVES], F32)
-        neg_scores = [sb("neg_scores%d" % h, [P, 2, SLOTS], F32) for h in range(HALVES)]
-        probs = [sb("probs%d" % h, [P, 2, SLOTS], F32) for h in range(HALVES)]
+        neg_scores = sb("neg_scores", [P, HALVES, 2, SLOTS], F32, reuse="ksp1")
+        probs = [sb("probs0", [P, 2, SLOTS], F32, reuse="vp11"),
+                 sb("probs1", [P, 2, SLOTS], F32)]
         for h in range(HALVES):
-            nc.vector.tensor_scalar(out=neg_scores[h][:, 0, :], in0=scores[0, h][:], scalar1=-1.0, scalar2=None,
+            nc.vector.tensor_scalar(out=neg_scores[:, h, 0, :], in0=scores[0, h][:], scalar1=-1.0, scalar2=None,
                                     op0=ALU.mult, op1=ALU.min, accum_out=neg_first[:, h:h + 1])
         for h in range(HALVES):
-            nc.vector.tensor_scalar(out=neg_scores[h][:, 1, :], in0=scores[1, h][:], scalar1=-1.0,
+            nc.vector.tensor_scalar(out=neg_scores[:, h, 1, :], in0=scores[1, h][:], scalar1=-1.0,
                                     scalar2=neg_first[:, h:h + 1], op0=ALU.mult, op1=ALU.min,
                                     accum_out=neg_max[:, h:h + 1])
-            nc.scalar.activation(out=probs[h][:], in_=neg_scores[h][:], func=ACT.Exp,
+            nc.scalar.activation(out=probs[h][:], in_=neg_scores[:, h], func=ACT.Exp,
                                  bias=neg_max[:, h:h + 1], scale=-1.0, accum_out=row_sum[:, h:h + 1])
-        values(0, 0)
-        cast("scalar", 1, reuse="neg_scores1")
-        values(1, 1)
+        spread = []
+        for c in range(2):
+            bank = psum.tile([P, SLOTS], F32, name="spread%d" % c, tag="big0%d" % c)
+            for t in range(PACK):
+                nc.tensor.transpose(bank[:, t::PACK], slot_w[c][:, t:t + 1].to_broadcast([P, P]), ident[:])
+            spread.append(bank)
+
+        turn_values(1, 0, first_picked)
+        values(0, 0, reuse="neg_first")
+        values(1, 1, reuse="ksp1")
         copy_out(0)
+        cast(2, reuse="cast1")
 
         w_grouped = []
         for h in range(HALVES):
             inv_sum = sb("inv_sum%d" % h, [P, 1], F32, reuse="vp00")
             nc.vector.reciprocal(out=inv_sum[:], in_=row_sum[:, h:h + 1])
-            bank = psum.tile([P, 2, 2, P], F32, name="wturn%d" % h, tag="big1%d" % h)
+            bank = psum.tile([P, 2, 2, P], F32, name="wturn%d" % h, tag="turn", bufs=TURN_BANKS)
             for c in range(2):
                 weights = sb("weights%d%d" % (c, h), [P, SLOTS], BF16)
                 nc.vector.scalar_tensor_tensor(out=weights[:], in0=probs[h][:, c, :], scalar=inv_sum[:],
@@ -179,7 +188,6 @@ def tile_attend_two_caches_pl_kernel(tc, query, keys_words, keys_scales, rkey_wo
                 turn(weights[:], bank[:, c])
             w_grouped.append(sb("wg%d" % h, [P, 2, P, 2], F32))
             nc.scalar.copy(out=w_grouped[h][:], in_=bank[:].rearrange("p c u q -> p c q u"))
-        cast("vector", 2)
         values(0, 1, reuse="probs1")
         copy_out(1)
         values(1, 2, reuse="probs1")
@@ -191,16 +199,16 @@ def tile_attend_two_caches_pl_kernel(tc, query, keys_words, keys_scales, rkey_wo
         for h in range(HALVES):
             nc.vector.quantize_mx(out=w_codes[:, h, :].bitcast(FP8X4), scales=w_scales[:, h, :],
                                   in_=w_grouped[h][:].rearrange("p c q u -> p (c q u)").bitcast(BF16))
-        scales = sb("vs", [P, 8 * P], U8)
-        quantize_values(early[:], GROUPS[0] + GROUPS[1], mid_codes[:, 1, :], scales[:, 0:4 * P])
+        all_v_scales = sb("vs", [P, 8 * P], U8)
+        quantize_values(early[:], GROUPS[0] + GROUPS[1], mid_codes[:, 1, :], all_v_scales[:, 0:4 * P])
         values(0, 3)
         copy_out(3)
         values(1, 3)
         copy_out(4)
-        codes = sb("vc_late", [P, 4 * P], U32, reuse="vp13")
-        quantize_values(v_grouped[2], GROUPS[2], codes[:, 0:2 * P], scales[:, 4 * P:6 * P])
-        quantize_values(v_grouped[3], GROUPS[3], codes[:, 2 * P:3 * P], scales[:, 6 * P:7 * P])
-        quantize_values(v_grouped[4], GROUPS[4], codes[:, 3 * P:4 * P], scales[:, 7 * P:8 * P])
+        late_codes = sb("vc_late", [P, 4 * P], U32, reuse="vp13")
+        quantize_values(v_grouped[2], GROUPS[2], late_codes[:, 0:2 * P], all_v_scales[:, 4 * P:6 * P])
+        quantize_values(v_grouped[3], GROUPS[3], late_codes[:, 2 * P:3 * P], all_v_scales[:, 6 * P:7 * P])
+        quantize_values(v_grouped[4], GROUPS[4], late_codes[:, 3 * P:4 * P], all_v_scales[:, 7 * P:8 * P])
 
         result = [psum.tile([P, PACK, P], F32, name="result%d" % h, tag="big0%d" % h) for h in range(HALVES)]
         out_sb = [sb("out_first", [P, 2, Q], F32), sb("out_last", [P, 2, Q], F32)]
@@ -230,7 +238,7 @@ def tile_attend_two_caches_pl_kernel(tc, query, keys_words, keys_scales, rkey_wo
             nc.vector.quantize_mx(out=o_codes[:, h * P:(h + 1) * P].bitcast(FP8X4), scales=o_scales[:, h * P:(h + 1) * P],
                                   in_=o_bf[h][:].rearrange("p q r -> p (q r)"))
         nc.scalar.dma_start(out=out_1[0].rearrange("p c t -> p (c t)").bitcast(I32), in_=o_codes[:].bitcast(I32))
-        for quad in range(4):
-            queue = nc.sync if quad < 2 else nc.scalar
+        for quad in range(QUADRANTS):
+            queue = nc.sync if quad < QUADRANTS // 2 else nc.scalar
             queue.dma_start(out=out_2[0, 4 * quad:4 * quad + 4, :].bitcast(I32),
                             in_=o_scales[32 * quad:32 * quad + 4, :].bitcast(I32))

@@ -1,7 +1,6 @@
 from contextlib import ExitStack
 
 import concourse.mybir as mybir
-from concourse.masks import make_identity
 
 F32 = mybir.dt.float32
 BF16 = mybir.dt.bfloat16
@@ -13,232 +12,268 @@ FP8X4 = mybir.dt.float8_e4m3fn_x4
 FP4X4 = mybir.dt.float4_e2m1fn_x4
 ACT = mybir.ActivationFunctionType
 ALU = mybir.AluOpType
+AX = mybir.AxisListType
 
 P = 128
 PACK = 4
-QUADRANTS = 4
 D, T, Q, E, U, SLOTS = 512, 2048, 256, 512, 1024, 512
 HALVES = Q // P
 FLOPS = 2 * 2 * D * Q * SLOTS + 2 * 2 * SLOTS * E * Q
-LOAD_ORDER = ((1, 0), (1, 1), (0, 0), (1, 2), (0, 1), (0, 2), (0, 3), (1, 3))
-GROUPS = (((1, 0), (0, 0)), ((1, 1), (0, 1)), ((0, 2), (1, 2)), ((0, 3),), ((1, 3),))
-TURN_BANKS = 4
+KIB = 1024
 
 
 def tile_attend_two_caches_pl_kernel(tc, query, keys_words, keys_scales, rkey_words, rkey_scales,
-                                      size, rsz, vals, rval, offs, offs2, out_0, out_1, out_2):
+                                         size, rsz, vals, rval, offs, offs2, out_0, out_1, out_2):
     nc = tc.nc
     with ExitStack() as ctx:
         keep = ctx.enter_context(tc.tile_pool(name="keep", bufs=1))
+        shared = ctx.enter_context(tc.tile_pool(name="shared", bufs=1))
         psum = ctx.enter_context(tc.psum_pool(name="psum", bufs=1))
 
-        def sb(name, shape, dtype, reuse=None):
-            return keep.tile(shape, dtype, name=name, tag=reuse or name, align_bytes=64)
+        def sb(name, shape, dtype, at=None):
+            if at is None:
+                return keep.tile(shape, dtype, name=name, align_bytes=64)
+            return shared.tile(shape, dtype, name=name, align_bytes=64, offset=int(at * KIB))
 
+        def bank(name, shape, number):
+            return psum.tile(shape, F32, name=name, tag="bank%d" % number)
+
+        LONG, RECENT = 0, 1
+        scale_row = (0, 4)
         lists = [keep.tile([P, SLOTS // 16], U16, name="list0"), keep.tile([P, SLOTS // 16], U16, name="list1")]
-        key_scale_pool = [sb("ksp0", [P, T], U8), sb("ksp1", [P, U], U8)]
-        key_word_pool = [sb("kwp0", [P, T], U16), sb("kwp1", [P, U], U32)]
-
-        nc.vector.memset(key_scale_pool[0][:].bitcast(I32), 0)
-        warm = sb("warm", [P, 2], F32)
-        nc.vector.memset(warm[:, 0:1], 0.0)
-        nc.vector.memset(key_scale_pool[1][:].bitcast(I32), 0)
-
-        def load_scales(c, src):
-            for quad in range(QUADRANTS):
-                nc.scalar.dma_start(out=key_scale_pool[c][32 * quad:32 * quad + 4, :].bitcast(I32),
-                                    in_=src[0, 4 * quad:4 * quad + 4, :].bitcast(I32))
-
-        nc.sync.dma_start(lists[0][:], offs)
-        nc.sync.dma_start(out=key_word_pool[0][:].bitcast(I32), in_=keys_words[0].bitcast(I32))
-        load_scales(0, keys_scales)
-        nc.scalar.activation(out=warm[:, 1:2], in_=warm[:, 0:1], func=ACT.Exp)
-        nc.sync.dma_start(lists[1][:], offs2)
-        nc.sync.dma_start(out=key_word_pool[1][:].bitcast(I32),
-                          in_=rkey_words[0].rearrange("p n t -> p (n t)").bitcast(I32))
-        q_raw = sb("q_raw", [P, PACK, Q], F32)
-        nc.sync.dma_start(out=q_raw[:], in_=query.rearrange("(p j) q -> p j q", j=PACK))
-        load_scales(1, rkey_scales)
-        slot_w = [sb("slot_w0", [P, PACK], F32), sb("slot_w1", [P, PACK], F32)]
-        for c, src in enumerate((size, rsz)):
-            nc.sync.dma_start(out=slot_w[c][:], in_=src.rearrange("o (p t) -> (o p) t", t=PACK))
         pools = (vals, rval)
         widths = (T, U)
-        val_pool = {}
-        for c, r in LOAD_ORDER:
-            val_pool[c, r] = sb("vp%d%d" % (c, r), [P, widths[c]], F32)
+        val_pool, key_scale_pool, key_word_pool = {}, {}, {}
+
+        def load_scales(c, src, at=None):
+            key_scale_pool[c] = sb("ksp%d" % c, [P, widths[c]], U8, at)
+            nc.vector.memset(key_scale_pool[c][:].bitcast(I32), 0)
+            rows = src[0].rearrange("(quad j) n -> j quad n", j=4)
+            for j in range(4):
+                nc.sync.dma_start(out=key_scale_pool[c][scale_row[c] + j:P:32, :].bitcast(I32), in_=rows[j].bitcast(I32))
+
+        def load_values(c, r, at):
+            val_pool[c, r] = sb("vp%d%d" % (c, r), [P, widths[c]], F32, at)
             nc.sync.dma_start(out=val_pool[c, r][:], in_=pools[c].rearrange("(m r) t -> r m t", r=PACK)[r])
 
-        ident = sb("ident", [P, P], F32)
-        make_identity(nc, ident[:])
+        nc.sync.dma_start(lists[RECENT][:], offs2)
+        nc.sync.dma_start(lists[LONG][:], offs)
+        key_word_pool[RECENT] = sb("kwp1", [P, U], U32)
+        nc.sync.dma_start(out=key_word_pool[RECENT][:].bitcast(I32),
+                          in_=rkey_words[0].rearrange("p n t -> p (n t)").bitcast(I32))
+        load_scales(RECENT, rkey_scales)
 
-        key_scales = [sb("ks0", [P, SLOTS], U8)]
+        ident = sb("ident", [P, P], F32)
+        zeros = sb("zeros", [P, P], F32)
+        nc.gpsimd.memset(zeros[:, 0:P], 0.0)
+        nc.gpsimd.affine_select(out=ident[:], in_=zeros[:, 0:P], compare_op=ALU.not_equal, fill=1.0, base=0,
+                                pattern=[[-1, P]], channel_multiplier=1)
+
+        q_raw = sb("q_raw", [P, PACK, Q], F32)
+        nc.sync.dma_start(out=q_raw[:], in_=query.rearrange("(p j) q -> p j q", j=PACK))
+        load_values(RECENT, 0, None)
+        load_scales(LONG, keys_scales)
+        warm = sb("warm", [P, 49 * KIB // 4], F32, at=10)
+        nc.vector.memset(warm[:, 0:1], 0.0)
+        nc.scalar.activation(out=warm[:, 1:2], in_=warm[:, 0:1], func=ACT.Exp)
+        key_word_pool[LONG] = sb("kwp0", [P, T], U16, at=11)
+        nc.sync.dma_start(out=key_word_pool[LONG][:].bitcast(I32), in_=keys_words[0].bitcast(I32))
+        load_values(RECENT, 1, at=15)
+        slot_w = [sb("slot_w0", [P, PACK], F32, at=10.25), sb("slot_w1", [P, PACK], F32, at=10.5)]
+        for k, src in enumerate((size, rsz)):
+            nc.sync.dma_start(out=slot_w[k][:], in_=src.rearrange("o (p t) -> (o p) t", t=PACK))
+        load_values(LONG, 0, at=27)
+        load_values(RECENT, 2, at=19)
+        load_values(LONG, 1, at=35)
+        load_values(RECENT, 3, at=23)
+        load_values(LONG, 2, at=43)
+        load_values(LONG, 3, at=51)
+
+        key_scales = [sb("ks0", [P, SLOTS], U8), sb("ks1", [P, SLOTS], U8)]
         key_words = [sb("kw0", [P, SLOTS], U16), sb("kw1", [P, SLOTS], U32)]
-        for c in range(2):
-            nc.vector.tensor_copy(key_words[c][:], key_word_pool[c][:].indirect(lists[c][:]))
-        nc.vector.tensor_copy(key_scales[0][:], key_scale_pool[0][:].indirect(lists[0][:]))
+        nc.vector.tensor_copy(key_words[RECENT][:], key_word_pool[RECENT][:].indirect(lists[RECENT][:]))
+        nc.vector.tensor_copy(key_scales[RECENT][:], key_scale_pool[RECENT][:].indirect(lists[RECENT][:]))
+        nc.vector.tensor_copy(key_scales[LONG][:], key_scale_pool[LONG][:].indirect(lists[LONG][:]))
+
         q_bf = sb("q_bf", [P, Q, PACK], BF16)
         nc.scalar.activation(out=q_bf[:].rearrange("p (c i) t -> p c t i", i=4),
                              in_=q_raw[:].rearrange("p t (c i) -> p c t i", i=4), func=ACT.Copy)
-        q_codes = sb("q_codes", [P, Q], U32, reuse="ksp0")
+        q_codes = sb("q_codes", [P, Q], U32)
         q_scales = sb("q_scales", [P, Q], U8)
         nc.vector.quantize_mx(out=q_codes[:].bitcast(FP8X4), scales=q_scales[:],
                               in_=q_bf[:].rearrange("p q t -> p (q t)"))
-        key_scales.append(sb("ks1", [P, SLOTS], U8, reuse="q_bf"))
-        nc.vector.tensor_copy(key_scales[1][:], key_scale_pool[1][:].indirect(lists[1][:]))
+        nc.vector.tensor_copy(key_words[LONG][:], key_word_pool[LONG][:].indirect(lists[LONG][:]))
 
-        key_formats = (FP4X4, FP8X4)
+        fmts = (FP4X4, FP8X4)
         scores = {}
-        for c in range(2):
+        for c in (RECENT, LONG):
             for h in range(HALVES):
-                scores[c, h] = psum.tile([P, SLOTS], F32, name="score%d%d" % (c, h), tag="big%d%d" % (c, h))
+                scores[c, h] = bank("score%d%d" % (c, h), [P, SLOTS], 2 * (1 - c) + h)
                 nc.tensor.matmul_mx(out=scores[c, h][:],
                                     lhsT=q_codes[:, h * P:(h + 1) * P].bitcast(FP8X4),
                                     lhsT_scale=q_scales[:, h * P:(h + 1) * P],
-                                    rhs=key_words[c][:].bitcast(key_formats[c]), rhs_scale=key_scales[c][:],
+                                    rhs=key_words[c][:].bitcast(fmts[c]), rhs_scale=key_scales[c][scale_row[c]:P, :],
                                     start=True, stop=True)
 
-        def turn(src_bf, bank):
+        casts = {}
+
+        def cast(r, on_vector=False, at=None):
+            casts[r] = sb("cast%d" % r, [P, U], BF16, at)
+            if on_vector:
+                nc.vector.tensor_copy(out=casts[r][:], in_=val_pool[RECENT, r][:])
+            else:
+                nc.scalar.activation(out=casts[r][:], in_=val_pool[RECENT, r][:], func=ACT.Copy)
+
+        def turn(src_bf, dst):
             words = src_bf.bitcast(F32)
             for u in range(2):
-                nc.tensor.transpose(bank[:, u, :], words[:, u::2], ident[:])
+                nc.tensor.transpose(dst[:, u, :], words[:, u::2], ident[:])
 
-        v_codes, v_scales = {}, {}
-        early = sb("vg_early", [P, 4, P, 2], F32)
-        v_grouped = [early[:, 0:2], early[:, 2:4]] + [sb("vg%d" % g, [P, len(GROUPS[g]), P, 2], F32)[:] for g in (2, 3, 4)]
-        place = {cr: (g, k) for g, group in enumerate(GROUPS) for k, cr in enumerate(group)}
-        banks, casts = {}, {}
-
-        def cast(r, reuse=None):
-            casts[r] = sb("cast%d" % r, [P, U], BF16, reuse=reuse)
-            nc.scalar.activation(out=casts[r][:], in_=val_pool[1, r][:], func=ACT.Copy)
-
-        def values(c, r, reuse=None):
-            turn_values(c, r, pick(c, r, reuse))
-
-        def pick(c, r, reuse=None):
-            picked = sb("picked%d%d" % (c, r), [P, SLOTS], BF16, reuse=reuse)
-            if c == 1 and r in casts:
+        def pick_and_turn(c, r, dst, at=None):
+            picked = sb("picked%d%d" % (c, r), [P, SLOTS], BF16, at)
+            if c == RECENT:
                 nc.scalar.activation(out=picked[:], in_=casts[r][:].indirect(lists[c][:]), func=ACT.Copy)
             else:
                 nc.vector.tensor_copy(picked[:], val_pool[c, r][:].indirect(lists[c][:]))
+            turn(picked[:], dst)
             return picked
 
-        def turn_values(c, r, picked):
-            g, k = place[c, r]
-            if g not in banks:
-                if g < HALVES:
-                    banks[g] = psum.tile([P, 2, 2, P], F32, name="vturn%d" % g, tag="big1%d" % g)
-                else:
-                    banks[g] = psum.tile([P, 2, 2, P], F32, name="vturn%d" % g, tag="turn", bufs=TURN_BANKS)
-            turn(picked[:], banks[g][:, k])
+        groups = (((RECENT, 0),), ((RECENT, 1), (LONG, 0)), ((RECENT, 2), (LONG, 1)), ((RECENT, 3), (LONG, 2)),
+                  ((LONG, 3),))
+        turned, v_grouped, v_codes, v_scales = {}, {}, {}, {}
 
-        def copy_out(g):
-            n = len(GROUPS[g])
-            nc.scalar.copy(out=v_grouped[g], in_=banks[g][:, 0:n].rearrange("p k u m -> p k m u"))
+        def open_turn(g, number):
+            turned[g] = bank("vturn%d" % g, [P, len(groups[g]), 2, P], number)
 
-        def quantize_values(src, members, codes, scales):
-            nc.vector.quantize_mx(out=codes.bitcast(FP8X4), scales=scales,
-                                  in_=src.rearrange("p k m u -> p (k m u)").bitcast(BF16))
-            for k, cr in enumerate(members):
+        def copy_out(g, at=None):
+            v_grouped[g] = sb("vg%d" % g, [P, len(groups[g]), P, 2], F32, at)
+            nc.scalar.copy(out=v_grouped[g][:], in_=turned[g][:].rearrange("p k u m -> p k m u"))
+
+        def quantize_values(g, at=None):
+            n = len(groups[g])
+            codes = sb("vc%d" % g, [P, n * P], U32, at)
+            scales = sb("vs%d" % g, [P, n * P], U8)
+            nc.vector.quantize_mx(out=codes[:].bitcast(FP8X4), scales=scales[:],
+                                  in_=v_grouped[g][:].rearrange("p k m u -> p (k m u)").bitcast(BF16))
+            for k, cr in enumerate(groups[g]):
                 v_codes[cr] = codes[:, k * P:(k + 1) * P]
                 v_scales[cr] = scales[:, k * P:(k + 1) * P]
 
         cast(0)
-        first_picked = pick(1, 0)
-        cast(1)
+        open_turn(0, 6)
+        pick_and_turn(RECENT, 0, turned[0][:, 0])
+        cast(1, at=74)
+        copy_out(0, at=15)
+        open_turn(1, 7)
+        pick_and_turn(RECENT, 1, turned[1][:, 0])
 
-        neg_first = sb("neg_first", [P, HALVES], F32)
+        neg_first = [sb("neg_first0", [P, 1], F32, at=11), sb("neg_first1", [P, 1], F32, at=12)]
         neg_max = sb("neg_max", [P, HALVES], F32)
-        row_sum = sb("row_sum", [P, HALVES], F32)
-        neg_scores = sb("neg_scores", [P, HALVES, 2, SLOTS], F32, reuse="ksp1")
-        probs = [sb("probs0", [P, 2, SLOTS], F32, reuse="vp11"),
-                 sb("probs1", [P, 2, SLOTS], F32)]
+        row_sum = [sb("row_sum0", [P, 1], F32, at=74), sb("row_sum1", [P, 1], F32, at=74.25)]
+        neg_scores = [sb("neg_scores0", [P, 2, SLOTS], F32, at=60), sb("neg_scores1", [P, 2, SLOTS], F32, at=64)]
+        probs = [sb("probs0", [P, 2, SLOTS], F32, at=0), sb("probs1", [P, 2, SLOTS], F32, at=4)]
         for h in range(HALVES):
-            nc.vector.tensor_scalar(out=neg_scores[:, h, 0, :], in0=scores[0, h][:], scalar1=-1.0, scalar2=None,
-                                    op0=ALU.mult, op1=ALU.min, accum_out=neg_first[:, h:h + 1])
+            nc.vector.tensor_scalar(out=neg_scores[h][:, RECENT, :], in0=scores[RECENT, h][:], scalar1=-1.0,
+                                    scalar2=None, op0=ALU.mult, op1=ALU.min, accum_out=neg_first[h][:])
         for h in range(HALVES):
-            nc.vector.tensor_scalar(out=neg_scores[:, h, 1, :], in0=scores[1, h][:], scalar1=-1.0,
-                                    scalar2=neg_first[:, h:h + 1], op0=ALU.mult, op1=ALU.min,
+            nc.vector.tensor_scalar(out=neg_scores[h][:, LONG, :], in0=scores[LONG, h][:], scalar1=-1.0,
+                                    scalar2=neg_first[h][:], op0=ALU.mult, op1=ALU.min,
                                     accum_out=neg_max[:, h:h + 1])
-            nc.scalar.activation(out=probs[h][:], in_=neg_scores[:, h], func=ACT.Exp,
-                                 bias=neg_max[:, h:h + 1], scale=-1.0, accum_out=row_sum[:, h:h + 1])
-        spread = []
-        for c in range(2):
-            bank = psum.tile([P, SLOTS], F32, name="spread%d" % c, tag="big0%d" % c)
+            nc.scalar.activation(out=probs[h][:], in_=neg_scores[h][:], func=ACT.Exp,
+                                 bias=neg_max[:, h:h + 1], scale=-1.0, accum_out=row_sum[h][:])
+        spread = {}
+        for c in (RECENT, LONG):
+            spread[c] = bank("spread%d" % c, [P, SLOTS], 4 + c)
             for t in range(PACK):
-                nc.tensor.transpose(bank[:, t::PACK], slot_w[c][:, t:t + 1].to_broadcast([P, P]), ident[:])
-            spread.append(bank)
+                nc.tensor.transpose(spread[c][:, t::PACK], slot_w[c][:, t:t + 1].to_broadcast([P, P]), ident[:])
 
-        turn_values(1, 0, first_picked)
-        values(0, 0, reuse="neg_first")
-        values(1, 1, reuse="ksp1")
-        copy_out(0)
-        cast(2, reuse="cast1")
+        pick_and_turn(LONG, 0, turned[1][:, 1], at=11)
+        cast(2, on_vector=True, at=12)
+        inv_sum = [sb("inv_sum%d" % h, [P, 1], F32) for h in range(HALVES)]
+        nc.vector.reciprocal(out=inv_sum[0][:], in_=row_sum[0][:])
+        quantize_values(0, at=60)
 
-        w_grouped = []
-        for h in range(HALVES):
-            inv_sum = sb("inv_sum%d" % h, [P, 1], F32, reuse="vp00")
-            nc.vector.reciprocal(out=inv_sum[:], in_=row_sum[:, h:h + 1])
-            bank = psum.tile([P, 2, 2, P], F32, name="wturn%d" % h, tag="turn", bufs=TURN_BANKS)
-            for c in range(2):
-                weights = sb("weights%d%d" % (c, h), [P, SLOTS], BF16)
-                nc.vector.scalar_tensor_tensor(out=weights[:], in0=probs[h][:, c, :], scalar=inv_sum[:],
-                                               in1=spread[c][:], op0=ALU.mult, op1=ALU.mult)
-                turn(weights[:], bank[:, c])
-            w_grouped.append(sb("wg%d" % h, [P, 2, P, 2], F32))
-            nc.scalar.copy(out=w_grouped[h][:], in_=bank[:].rearrange("p c u q -> p c q u"))
-        values(0, 1, reuse="probs1")
-        copy_out(1)
-        values(1, 2, reuse="probs1")
-        values(0, 2)
-        copy_out(2)
-        mid_codes = sb("mid_codes", [P, 2, 4 * P], U32, reuse="vp02")
-        w_codes = mid_codes[:, 0, :].rearrange("p (h n) -> p h n", h=HALVES)
-        w_scales = sb("ws", [P, HALVES, 2 * P], U8)
-        for h in range(HALVES):
-            nc.vector.quantize_mx(out=w_codes[:, h, :].bitcast(FP8X4), scales=w_scales[:, h, :],
+        w_turned = [bank("wturn%d" % h, [P, 2, 2, P], h) for h in range(HALVES)]
+        w_grouped, w_codes, w_scales = {}, {}, {}
+
+        def weigh(h, c, at=None):
+            weights = sb("weights%d%d" % (c, h), [P, SLOTS], BF16, at)
+            nc.vector.scalar_tensor_tensor(out=weights[:], in0=probs[h][:, c, :], scalar=inv_sum[h][:],
+                                           in1=spread[c][:], op0=ALU.mult, op1=ALU.mult)
+            turn(weights[:], w_turned[h][:, c])
+            return weights
+
+        def copy_weights(h, at):
+            w_grouped[h] = sb("wg%d" % h, [P, 2, P, 2], F32, at)
+            nc.scalar.copy(out=w_grouped[h][:], in_=w_turned[h][:].rearrange("p c u q -> p c q u"))
+
+        def quantize_weights(h, at=None):
+            w_codes[h] = sb("wc%d" % h, [P, 2 * P], U32, at)
+            w_scales[h] = sb("ws%d" % h, [P, 2 * P], U8)
+            nc.vector.quantize_mx(out=w_codes[h][:].bitcast(FP8X4), scales=w_scales[h][:],
                                   in_=w_grouped[h][:].rearrange("p c q u -> p (c q u)").bitcast(BF16))
-        all_v_scales = sb("vs", [P, 8 * P], U8)
-        quantize_values(early[:], GROUPS[0] + GROUPS[1], mid_codes[:, 1, :], all_v_scales[:, 0:4 * P])
-        values(0, 3)
-        copy_out(3)
-        values(1, 3)
-        copy_out(4)
-        late_codes = sb("vc_late", [P, 4 * P], U32, reuse="vp13")
-        quantize_values(v_grouped[2], GROUPS[2], late_codes[:, 0:2 * P], all_v_scales[:, 4 * P:6 * P])
-        quantize_values(v_grouped[3], GROUPS[3], late_codes[:, 2 * P:3 * P], all_v_scales[:, 6 * P:7 * P])
-        quantize_values(v_grouped[4], GROUPS[4], late_codes[:, 3 * P:4 * P], all_v_scales[:, 7 * P:8 * P])
 
-        result = [psum.tile([P, PACK, P], F32, name="result%d" % h, tag="big0%d" % h) for h in range(HALVES)]
-        out_sb = [sb("out_first", [P, 2, Q], F32), sb("out_last", [P, 2, Q], F32)]
+        w0b = weigh(0, RECENT, at=72)
+        nc.vector.reciprocal(out=inv_sum[1][:], in_=row_sum[1][:])
+        weigh(0, LONG, at=68)
+        copy_out(1, at=64)
+        open_turn(2, 2)
+        pick_and_turn(RECENT, 2, turned[2][:, 0], at=72)
+        copy_weights(0, at=19)
+        weigh(1, RECENT)
+        weigh(1, LONG, at=70)
+        cast(3, at=68)
+        copy_weights(1, at=23)
+        pick_and_turn(LONG, 1, turned[2][:, 1], at=0)
+        quantize_values(1, at=4)
+        quantize_weights(0)
+        open_turn(3, 3)
+        pick_and_turn(RECENT, 3, turned[3][:, 0], at=70)
+        pick_and_turn(LONG, 2, turned[3][:, 1], at=5)
+        quantize_weights(1, at=43)
+        copy_out(2, at=25)
+        copy_out(3)
+
+        result = [bank("result%d" % h, [P, PACK, P], 4 + h) for h in range(HALVES)]
+        out_sb = [sb("out_first", [P, 1, Q], F32, at=44), sb("out_last", [P, 3, Q], F32)]
         out_rows = out_0.rearrange("(p r) q -> p r q", r=PACK)
-        for r in range(PACK):
-            for c in range(2):
-                for h in range(HALVES):
+
+        def multiply(r):
+            for h in range(HALVES):
+                for c in (RECENT, LONG):
                     nc.tensor.matmul_mx(out=result[h][:, r, :],
                                         lhsT=v_codes[c, r].bitcast(FP8X4), lhsT_scale=v_scales[c, r],
-                                        rhs=w_codes[:, h, c * P:(c + 1) * P].bitcast(FP8X4),
-                                        rhs_scale=w_scales[:, h, c * P:(c + 1) * P],
-                                        start=(c == 0), stop=(c == 1))
-            if r == 1:
-                for h in range(HALVES):
-                    nc.scalar.copy(out=out_sb[0][:, :, h * P:(h + 1) * P], in_=result[h][:, 0:2, :])
-                nc.sync.dma_start(out=out_rows[:, 0:2, :], in_=out_sb[0][:])
+                                        rhs=w_codes[h][:, c * P:(c + 1) * P].bitcast(FP8X4),
+                                        rhs_scale=w_scales[h][:, c * P:(c + 1) * P],
+                                        start=(c == RECENT), stop=(c == LONG))
+
+        multiply(0)
+        for h in range(HALVES):
+            nc.scalar.copy(out=out_sb[0][:, :, h * P:(h + 1) * P], in_=result[h][:, 0:1, :])
+        nc.sync.dma_start(out=out_rows[:, 0:1, :], in_=out_sb[0][:])
+        open_turn(4, 6)
+        pk3 = pick_and_turn(LONG, 3, turned[4][:, 0])
+        quantize_values(2, at=51)
+        quantize_values(3, at=52)
+        copy_out(4)
+        multiply(1)
+        multiply(2)
+        quantize_values(4)
+        multiply(3)
 
         o_codes = sb("o_codes", [P, Q], U32)
         o_scales = sb("o_scales", [P, Q], U8)
         o_bf = [sb("o_bf%d" % h, [P, P, PACK], BF16) for h in range(HALVES)]
         nc.vector.tensor_copy(out=o_bf[0][:], in_=result[0][:].rearrange("p r q -> p q r"))
         nc.scalar.copy(out=o_bf[1][:], in_=result[1][:].rearrange("p r q -> p q r"))
-        nc.vector.tensor_copy(out=out_sb[1][:, :, 0:P], in_=result[0][:, 2:4, :])
-        nc.scalar.copy(out=out_sb[1][:, :, P:Q], in_=result[1][:, 2:4, :])
-        nc.sync.dma_start(out=out_rows[:, 2:4, :], in_=out_sb[1][:])
+        nc.vector.tensor_copy(out=out_sb[1][:, :, 0:P], in_=result[0][:, 1:4, :])
+        nc.scalar.copy(out=out_sb[1][:, :, P:Q], in_=result[1][:, 1:4, :])
+        nc.scalar.dma_start(out=out_rows[:, 1:4, :], in_=out_sb[1][:])
         for h in range(HALVES):
             nc.vector.quantize_mx(out=o_codes[:, h * P:(h + 1) * P].bitcast(FP8X4), scales=o_scales[:, h * P:(h + 1) * P],
                                   in_=o_bf[h][:].rearrange("p q r -> p (q r)"))
-        nc.scalar.dma_start(out=out_1[0].rearrange("p c t -> p (c t)").bitcast(I32), in_=o_codes[:].bitcast(I32))
-        for quad in range(QUADRANTS):
-            queue = nc.sync if quad < QUADRANTS // 2 else nc.scalar
+        nc.sync.dma_start(out=out_1[0].rearrange("p c t -> p (c t)").bitcast(I32), in_=o_codes[:].bitcast(I32))
+        for quad in range(4):
+            queue = nc.sync if quad < 3 else nc.scalar
             queue.dma_start(out=out_2[0, 4 * quad:4 * quad + 4, :].bitcast(I32),
                             in_=o_scales[32 * quad:32 * quad + 4, :].bitcast(I32))

@@ -194,7 +194,7 @@ def tile_attend_two_caches_pl_kernel(tc, query, keys_words, keys_scales, rkey_wo
         quantize_values(0, at=60)
 
         w_turned = [bank("wturn%d" % h, [P, 2, 2, P], h) for h in range(HALVES)]
-        w_grouped, w_codes, w_scales = {}, {}, {}
+        w_grouped = sb("wg", [P, 2, HALVES, P, 2], F32, at=21)
 
         def weigh(h, c, at=None):
             weights = sb("weights%d%d" % (c, h), [P, SLOTS], BF16, at)
@@ -203,15 +203,8 @@ def tile_attend_two_caches_pl_kernel(tc, query, keys_words, keys_scales, rkey_wo
             turn(weights[:], w_turned[h][:, c])
             return weights
 
-        def copy_weights(h, at):
-            w_grouped[h] = sb("wg%d" % h, [P, 2, P, 2], F32, at)
-            nc.scalar.copy(out=w_grouped[h][:], in_=w_turned[h][:].rearrange("p c u q -> p c q u"))
-
-        def quantize_weights(h, at=None):
-            w_codes[h] = sb("wc%d" % h, [P, 2 * P], U32, at)
-            w_scales[h] = sb("ws%d" % h, [P, 2 * P], U8)
-            nc.vector.quantize_mx(out=w_codes[h][:].bitcast(FP8X4), scales=w_scales[h][:],
-                                  in_=w_grouped[h][:].rearrange("p c q u -> p (c q u)").bitcast(BF16))
+        def copy_weights(h):
+            nc.scalar.copy(out=w_grouped[:, :, h], in_=w_turned[h][:].rearrange("p c u q -> p c q u"))
 
         w0b = weigh(0, RECENT, at=72)
         nc.vector.reciprocal(out=inv_sum[1][:], in_=row_sum[1][:])
@@ -219,56 +212,61 @@ def tile_attend_two_caches_pl_kernel(tc, query, keys_words, keys_scales, rkey_wo
         copy_out(1, at=64)
         open_turn(2, 2)
         pick_and_turn(RECENT, 2, turned[2][:, 0], at=72)
-        copy_weights(0, at=19)
         weigh(1, RECENT)
+        quantize_values(1, at=1)
         weigh(1, LONG, at=70)
         cast(3, at=68)
-        copy_weights(1, at=23)
+        copy_weights(0)
+        copy_weights(1)
         pick_and_turn(LONG, 1, turned[2][:, 1], at=0)
-        quantize_values(1, at=4)
-        quantize_weights(0)
         open_turn(3, 3)
         pick_and_turn(RECENT, 3, turned[3][:, 0], at=70)
         pick_and_turn(LONG, 2, turned[3][:, 1], at=5)
-        quantize_weights(1, at=43)
+        w_codes = sb("wc", [P, 2, Q], U32, at=43)
+        w_scales = sb("ws", [P, 2, Q], U8)
+        nc.vector.quantize_mx(out=w_codes[:].rearrange("p c q -> p (c q)").bitcast(FP8X4),
+                              scales=w_scales[:].rearrange("p c q -> p (c q)"),
+                              in_=w_grouped[:].rearrange("p c h q u -> p (c h q u)").bitcast(BF16))
         copy_out(2, at=25)
         copy_out(3)
 
-        result = [bank("result%d" % h, [P, PACK, P], 4 + h) for h in range(HALVES)]
-        out_sb = [sb("out_first", [P, 1, Q], F32, at=44), sb("out_last", [P, 3, Q], F32)]
+        result = [bank("result%d" % r, [P, Q], number) for r, number in enumerate((4, 5, 0, 1))]
+        out_sb = sb("out_sb", [P, PACK, Q], F32, at=76)
         out_rows = out_0.rearrange("(p r) q -> p r q", r=PACK)
 
-        def multiply(r):
-            for h in range(HALVES):
-                for c in (RECENT, LONG):
-                    nc.tensor.matmul_mx(out=result[h][:, r, :],
-                                        lhsT=v_codes[c, r].bitcast(FP8X4), lhsT_scale=v_scales[c, r],
-                                        rhs=w_codes[h][:, c * P:(c + 1) * P].bitcast(FP8X4),
-                                        rhs_scale=w_scales[h][:, c * P:(c + 1) * P],
-                                        start=(c == RECENT), stop=(c == LONG))
+        def multiply(c, r, start):
+            nc.tensor.matmul_mx(out=result[r][:], lhsT=v_codes[c, r].bitcast(FP8X4), lhsT_scale=v_scales[c, r],
+                                rhs=w_codes[:, c, :].bitcast(FP8X4), rhs_scale=w_scales[:, c, :],
+                                start=start, stop=not start)
 
-        multiply(0)
-        for h in range(HALVES):
-            nc.scalar.copy(out=out_sb[0][:, :, h * P:(h + 1) * P], in_=result[h][:, 0:1, :])
-        nc.sync.dma_start(out=out_rows[:, 0:1, :], in_=out_sb[0][:])
+        multiply(RECENT, 0, True)
+        multiply(LONG, 0, False)
         open_turn(4, 6)
         pk3 = pick_and_turn(LONG, 3, turned[4][:, 0])
         quantize_values(2, at=51)
         quantize_values(3, at=52)
-        copy_out(4)
-        multiply(1)
-        multiply(2)
+        copy_out(4, at=76)
+        for r in (1, 2):
+            multiply(LONG, r, True)
+            multiply(RECENT, r, False)
+        multiply(RECENT, 3, True)
         quantize_values(4)
-        multiply(3)
+        multiply(LONG, 3, False)
+        for r in range(2):
+            nc.scalar.copy(out=out_sb[:, r, :], in_=result[r][:])
+        nc.sync.dma_start(out=out_rows[:, 0:2, :], in_=out_sb[:, 0:2, :])
+        nc.vector.tensor_copy(out=out_sb[:, 2, :], in_=result[2][:])
+        nc.vector.tensor_copy(out=out_sb[:, 3, 0:P], in_=result[3][:, 0:P])
+        nc.scalar.copy(out=out_sb[:, 3, P:Q], in_=result[3][:, P:Q])
+        nc.sync.dma_start(out=out_rows[:, 2:4, :], in_=out_sb[:, 2:4, :])
 
         o_codes = sb("o_codes", [P, Q], U32)
         o_scales = sb("o_scales", [P, Q], U8)
         o_bf = [sb("o_bf%d" % h, [P, P, PACK], BF16) for h in range(HALVES)]
-        nc.vector.tensor_copy(out=o_bf[0][:], in_=result[0][:].rearrange("p r q -> p q r"))
-        nc.scalar.copy(out=o_bf[1][:], in_=result[1][:].rearrange("p r q -> p q r"))
-        nc.vector.tensor_copy(out=out_sb[1][:, :, 0:P], in_=result[0][:, 1:4, :])
-        nc.scalar.copy(out=out_sb[1][:, :, P:Q], in_=result[1][:, 1:4, :])
-        nc.scalar.dma_start(out=out_rows[:, 1:4, :], in_=out_sb[1][:])
+        nc.vector.tensor_copy(out=o_bf[0][:].rearrange("p (c i) r -> p c r i", i=4),
+                              in_=out_sb[:, :, 0:P].rearrange("p r (c i) -> p c r i", i=4))
+        nc.scalar.copy(out=o_bf[1][:].rearrange("p (c i) r -> p c r i", i=4),
+                       in_=out_sb[:, :, P:Q].rearrange("p r (c i) -> p c r i", i=4))
         for h in range(HALVES):
             nc.vector.quantize_mx(out=o_codes[:, h * P:(h + 1) * P].bitcast(FP8X4), scales=o_scales[:, h * P:(h + 1) * P],
                                   in_=o_bf[h][:].rearrange("p q r -> p (q r)"))

@@ -147,7 +147,8 @@ def tile_attend_two_caches_pl_kernel(tc, query, keys_words, keys_scales, rkey_wo
 
         def copy_out(g, at=None):
             v_grouped[g] = sb("vg%d" % g, [P, len(groups[g]), P, 2], F32, at)
-            nc.scalar.copy(out=v_grouped[g][:], in_=turned[g][:].rearrange("p k u m -> p k m u"))
+            nc.scalar.copy(out=v_grouped[g][:].rearrange("p k (m i) u -> p k m u i", i=2),
+                           in_=turned[g][:].rearrange("p k u (m i) -> p k m u i", i=2))
 
         def quantize_values(g, at=None):
             n = len(groups[g])
@@ -204,7 +205,8 @@ def tile_attend_two_caches_pl_kernel(tc, query, keys_words, keys_scales, rkey_wo
             return weights
 
         def copy_weights(h):
-            nc.scalar.copy(out=w_grouped[:, :, h], in_=w_turned[h][:].rearrange("p c u q -> p c q u"))
+            nc.scalar.copy(out=w_grouped[:, :, h].rearrange("p c (q i) u -> p c q u i", i=2),
+                           in_=w_turned[h][:].rearrange("p c u (q i) -> p c q u i", i=2))
 
         w0b = weigh(0, RECENT, at=72)
         nc.vector.reciprocal(out=inv_sum[1][:], in_=row_sum[1][:])

@@ -56,8 +56,14 @@ def tile_attend_two_caches_pl_kernel(tc, query, keys_words, keys_scales, rkey_wo
             val_pool[c, r] = sb("vp%d%d" % (c, r), [P, widths[c]], F32, at)
             nc.sync.dma_start(out=val_pool[c, r][:], in_=pools[c].rearrange("(m r) t -> r m t", r=PACK)[r])
 
+        slot_w = {}
+
+        def load_slot_weights(c, at=None):
+            slot_w[c] = sb("slot_w%d" % c, [P, PACK], F32, at)
+            nc.sync.dma_start(out=slot_w[c][:], in_=(size, rsz)[c].rearrange("o (p t) -> (o p) t", t=PACK))
+
         nc.sync.dma_start(lists[RECENT][:], offs2)
-        nc.sync.dma_start(lists[LONG][:], offs)
+        load_slot_weights(LONG)
         key_word_pool[RECENT] = sb("kwp1", [P, U], U32)
         nc.sync.dma_start(out=key_word_pool[RECENT][:].bitcast(I32),
                           in_=rkey_words[0].rearrange("p n t -> p (n t)").bitcast(I32))
@@ -72,6 +78,7 @@ def tile_attend_two_caches_pl_kernel(tc, query, keys_words, keys_scales, rkey_wo
         q_raw = sb("q_raw", [P, PACK, Q], F32)
         nc.sync.dma_start(out=q_raw[:], in_=query.rearrange("(p j) q -> p j q", j=PACK))
         load_values(RECENT, 0, None)
+        nc.sync.dma_start(lists[LONG][:], offs)
         load_scales(LONG, keys_scales)
         warm = sb("warm", [P, 49 * KIB // 4], F32, at=10)
         nc.vector.memset(warm[:, 0:1], 0.0)
@@ -79,9 +86,7 @@ def tile_attend_two_caches_pl_kernel(tc, query, keys_words, keys_scales, rkey_wo
         key_word_pool[LONG] = sb("kwp0", [P, T], U16, at=11)
         nc.sync.dma_start(out=key_word_pool[LONG][:].bitcast(I32), in_=keys_words[0].bitcast(I32))
         load_values(RECENT, 1, at=15)
-        slot_w = [sb("slot_w0", [P, PACK], F32, at=10.25), sb("slot_w1", [P, PACK], F32, at=10.5)]
-        for k, src in enumerate((size, rsz)):
-            nc.sync.dma_start(out=slot_w[k][:], in_=src.rearrange("o (p t) -> (o p) t", t=PACK))
+        load_slot_weights(RECENT, at=10.5)
         load_values(LONG, 0, at=27)
         load_values(RECENT, 2, at=19)
         load_values(LONG, 1, at=35)
@@ -124,17 +129,20 @@ def tile_attend_two_caches_pl_kernel(tc, query, keys_words, keys_scales, rkey_wo
             else:
                 nc.scalar.activation(out=casts[r][:], in_=val_pool[RECENT, r][:], func=ACT.Copy)
 
+        def dealt(ap):
+            return ap.rearrange("p (u b i) -> p b u i", u=2, i=16)
+
         def turn(src_bf, dst):
             words = src_bf.bitcast(F32)
             for u in range(2):
-                nc.tensor.transpose(dst[:, u, :], words[:, u::2], ident[:])
+                nc.tensor.transpose(dst[:, u, :], words[:, u * P:(u + 1) * P], ident[:])
 
         def pick_and_turn(c, r, dst, at=None):
             picked = sb("picked%d%d" % (c, r), [P, SLOTS], BF16, at)
             if c == RECENT:
-                nc.scalar.activation(out=picked[:], in_=casts[r][:].indirect(lists[c][:]), func=ACT.Copy)
+                nc.scalar.activation(out=dealt(picked[:]), in_=casts[r][:].indirect(lists[c][:]), func=ACT.Copy)
             else:
-                nc.vector.tensor_copy(picked[:], val_pool[c, r][:].indirect(lists[c][:]))
+                nc.vector.tensor_copy(dealt(picked[:]), val_pool[c, r][:].indirect(lists[c][:]))
             turn(picked[:], dst)
             return picked
 
@@ -147,8 +155,7 @@ def tile_attend_two_caches_pl_kernel(tc, query, keys_words, keys_scales, rkey_wo
 
         def copy_out(g, at=None):
             v_grouped[g] = sb("vg%d" % g, [P, len(groups[g]), P, 2], F32, at)
-            nc.scalar.copy(out=v_grouped[g][:].rearrange("p k (m i) u -> p k m u i", i=2),
-                           in_=turned[g][:].rearrange("p k u (m i) -> p k m u i", i=2))
+            nc.scalar.copy(out=v_grouped[g][:], in_=turned[g][:].rearrange("p k u m -> p k m u"))
 
         def quantize_values(g, at=None):
             n = len(groups[g])
@@ -174,10 +181,10 @@ def tile_attend_two_caches_pl_kernel(tc, query, keys_words, keys_scales, rkey_wo
         neg_scores = [sb("neg_scores0", [P, 2, SLOTS], F32, at=60), sb("neg_scores1", [P, 2, SLOTS], F32, at=64)]
         probs = [sb("probs0", [P, 2, SLOTS], F32, at=0), sb("probs1", [P, 2, SLOTS], F32, at=4)]
         for h in range(HALVES):
-            nc.vector.tensor_scalar(out=neg_scores[h][:, RECENT, :], in0=scores[RECENT, h][:], scalar1=-1.0,
+            nc.vector.tensor_scalar(out=dealt(neg_scores[h][:, RECENT, :]), in0=scores[RECENT, h][:].rearrange("p (b u i) -> p b u i", u=2, i=16), scalar1=-1.0,
                                     scalar2=None, op0=ALU.mult, op1=ALU.min, accum_out=neg_first[h][:])
         for h in range(HALVES):
-            nc.vector.tensor_scalar(out=neg_scores[h][:, LONG, :], in0=scores[LONG, h][:], scalar1=-1.0,
+            nc.vector.tensor_scalar(out=dealt(neg_scores[h][:, LONG, :]), in0=scores[LONG, h][:].rearrange("p (b u i) -> p b u i", u=2, i=16), scalar1=-1.0,
                                     scalar2=neg_first[h][:], op0=ALU.mult, op1=ALU.min,
                                     accum_out=neg_max[:, h:h + 1])
             nc.scalar.activation(out=probs[h][:], in_=neg_scores[h][:], func=ACT.Exp,
@@ -186,7 +193,7 @@ def tile_attend_two_caches_pl_kernel(tc, query, keys_words, keys_scales, rkey_wo
         for c in (RECENT, LONG):
             spread[c] = bank("spread%d" % c, [P, SLOTS], 4 + c)
             for t in range(PACK):
-                nc.tensor.transpose(spread[c][:, t::PACK], slot_w[c][:, t:t + 1].to_broadcast([P, P]), ident[:])
+                nc.tensor.transpose(spread[c][:].rearrange("p (u b j t) -> p t b u j", u=2, j=4, t=PACK)[:, t], slot_w[c][:, t:t + 1].to_broadcast([P, P]), ident[:])
 
         pick_and_turn(LONG, 0, turned[1][:, 1], at=11)
         cast(2, on_vector=True, at=12)
@@ -205,8 +212,7 @@ def tile_attend_two_caches_pl_kernel(tc, query, keys_words, keys_scales, rkey_wo
             return weights
 
         def copy_weights(h):
-            nc.scalar.copy(out=w_grouped[:, :, h].rearrange("p c (q i) u -> p c q u i", i=2),
-                           in_=w_turned[h][:].rearrange("p c u (q i) -> p c q u i", i=2))
+            nc.scalar.copy(out=w_grouped[:, :, h], in_=w_turned[h][:].rearrange("p c u q -> p c q u"))
 
         w0b = weigh(0, RECENT, at=72)
         nc.vector.reciprocal(out=inv_sum[1][:], in_=row_sum[1][:])
@@ -232,34 +238,38 @@ def tile_attend_two_caches_pl_kernel(tc, query, keys_words, keys_scales, rkey_wo
         copy_out(2, at=25)
         copy_out(3)
 
-        result = [bank("result%d" % r, [P, Q], number) for r, number in enumerate((4, 5, 0, 1))]
-        out_sb = sb("out_sb", [P, PACK, Q], F32, at=76)
+        early = bank("early", [P, 2, Q], 4)
+        third = bank("third", [P, Q], 5)
+        last = [bank("last%d" % h, [P, P], h) for h in range(HALVES)]
+        out_sb = sb("out_sb", [P, PACK, Q], F32)
         out_rows = out_0.rearrange("(p r) q -> p r q", r=PACK)
+        halves = [slice(h * P, (h + 1) * P) for h in range(HALVES)]
 
-        def multiply(c, r, start):
-            nc.tensor.matmul_mx(out=result[r][:], lhsT=v_codes[c, r].bitcast(FP8X4), lhsT_scale=v_scales[c, r],
-                                rhs=w_codes[:, c, :].bitcast(FP8X4), rhs_scale=w_scales[:, c, :],
+        def multiply(dst, c, r, start, columns=slice(0, Q)):
+            nc.tensor.matmul_mx(out=dst, lhsT=v_codes[c, r].bitcast(FP8X4), lhsT_scale=v_scales[c, r],
+                                rhs=w_codes[:, c, columns].bitcast(FP8X4), rhs_scale=w_scales[:, c, columns],
                                 start=start, stop=not start)
 
-        multiply(RECENT, 0, True)
-        multiply(LONG, 0, False)
+        multiply(early[:, 0, :], RECENT, 0, True)
+        multiply(early[:, 0, :], LONG, 0, False)
         open_turn(4, 6)
         pk3 = pick_and_turn(LONG, 3, turned[4][:, 0])
         quantize_values(2, at=51)
         quantize_values(3, at=52)
-        copy_out(4, at=76)
-        for r in (1, 2):
-            multiply(LONG, r, True)
-            multiply(RECENT, r, False)
-        multiply(RECENT, 3, True)
+        copy_out(4)
+        for r, dst in ((1, early[:, 1, :]), (2, third[:])):
+            multiply(dst, LONG, r, True)
+            multiply(dst, RECENT, r, False)
+        for h in range(HALVES):
+            multiply(last[h][:], RECENT, 3, True, halves[h])
         quantize_values(4)
-        multiply(LONG, 3, False)
-        for r in range(2):
-            nc.scalar.copy(out=out_sb[:, r, :], in_=result[r][:])
+        for h in range(HALVES):
+            multiply(last[h][:], LONG, 3, False, halves[h])
+        nc.scalar.copy(out=out_sb[:, 0:2, :], in_=early[:])
         nc.sync.dma_start(out=out_rows[:, 0:2, :], in_=out_sb[:, 0:2, :])
-        nc.vector.tensor_copy(out=out_sb[:, 2, :], in_=result[2][:])
-        nc.vector.tensor_copy(out=out_sb[:, 3, 0:P], in_=result[3][:, 0:P])
-        nc.scalar.copy(out=out_sb[:, 3, P:Q], in_=result[3][:, P:Q])
+        nc.vector.tensor_copy(out=out_sb[:, 2, :], in_=third[:])
+        nc.vector.tensor_copy(out=out_sb[:, 3, 0:P], in_=last[0][:])
+        nc.scalar.copy(out=out_sb[:, 3, P:Q], in_=last[1][:])
         nc.sync.dma_start(out=out_rows[:, 2:4, :], in_=out_sb[:, 2:4, :])
 
         o_codes = sb("o_codes", [P, Q], U32)
@@ -274,6 +284,6 @@ def tile_attend_two_caches_pl_kernel(tc, query, keys_words, keys_scales, rkey_wo
                                   in_=o_bf[h][:].rearrange("p q r -> p (q r)"))
         nc.sync.dma_start(out=out_1[0].rearrange("p c t -> p (c t)").bitcast(I32), in_=o_codes[:].bitcast(I32))
         for quad in range(4):
-            queue = nc.sync if quad < 3 else nc.scalar
+            queue = nc.sync if quad < 2 else nc.scalar
             queue.dma_start(out=out_2[0, 4 * quad:4 * quad + 4, :].bitcast(I32),
                             in_=o_scales[32 * quad:32 * quad + 4, :].bitcast(I32))

@@ -226,6 +226,11 @@ def tile_attend_two_caches_pl_kernel(tc, query, keys_words, keys_scales, rkey_wo
         cast(3, at=68)
         copy_weights(0)
         copy_weights(1)
+        idle = bank("idle", [P, SLOTS], 1)
+        for first in (True, False):
+            nc.tensor.matmul_mx(out=idle[:], lhsT=q_codes[:, 0:P].bitcast(FP8X4), lhsT_scale=q_scales[:, 0:P],
+                                rhs=key_words[RECENT][:].bitcast(FP8X4),
+                                rhs_scale=key_scales[RECENT][scale_row[RECENT]:P, :], start=first, stop=not first)
         pick_and_turn(LONG, 1, turned[2][:, 1], at=0)
         open_turn(3, 3)
         pick_and_turn(RECENT, 3, turned[3][:, 0], at=70)

@@ -12,14 +12,15 @@ FP8X4 = mybir.dt.float8_e4m3fn_x4
 FP4X4 = mybir.dt.float4_e2m1fn_x4
 ACT = mybir.ActivationFunctionType
 ALU = mybir.AluOpType
-AX = mybir.AxisListType
 
 P = 128
 PACK = 4
 D, T, Q, E, U, SLOTS = 512, 2048, 256, 512, 1024, 512
 HALVES = Q // P
 FLOPS = 2 * 2 * D * Q * SLOTS + 2 * 2 * SLOTS * E * Q
-KIB = 1024
+BYTES_OF = {F32: 4, U32: 4, BF16: 2, U16: 2, U8: 1}
+LONG, RECENT = 0, 1
+SHARE = 352
 
 
 def tile_attend_two_caches_pl_kernel(tc, query, keys_words, keys_scales, rkey_words, rkey_scales,
@@ -27,39 +28,43 @@ def tile_attend_two_caches_pl_kernel(tc, query, keys_words, keys_scales, rkey_wo
     nc = tc.nc
     with ExitStack() as ctx:
         keep = ctx.enter_context(tc.tile_pool(name="keep", bufs=1))
-        shared = ctx.enter_context(tc.tile_pool(name="shared", bufs=1))
+        work = ctx.enter_context(tc.tile_pool(name="work", bufs=1))
         psum = ctx.enter_context(tc.psum_pool(name="psum", bufs=1))
+        place = {"free": 0}
 
-        def sb(name, shape, dtype, at=None):
-            if at is None:
-                return keep.tile(shape, dtype, name=name, align_bytes=64)
-            return shared.tile(shape, dtype, name=name, align_bytes=64, offset=int(at * KIB))
+        def sb(name, shape, dtype, on=None, skip=0):
+            if on is None:
+                nbytes = BYTES_OF[dtype]
+                for n in shape[1:]:
+                    nbytes = nbytes * n
+                place[name] = place["free"]
+                place["free"] = place["free"] + (nbytes + 63) // 64 * 64
+            else:
+                place[name] = place[on] + skip
+            return work.tile(shape, dtype, name=name, align_bytes=64, offset=place[name])
 
         def bank(name, shape, number):
             return psum.tile(shape, F32, name=name, tag="bank%d" % number)
 
-        LONG, RECENT = 0, 1
         scale_row = (0, 4)
         lists = [keep.tile([P, SLOTS // 16], U16, name="list0"), keep.tile([P, SLOTS // 16], U16, name="list1")]
         pools = (vals, rval)
         widths = (T, U)
-        val_pool, key_scale_pool, key_word_pool = {}, {}, {}
+        val_pool, key_scale_pool, key_word_pool, slot_w = {}, {}, {}, {}
 
-        def load_scales(c, src, at=None):
-            key_scale_pool[c] = sb("ksp%d" % c, [P, widths[c]], U8, at)
+        def load_scales(c, src):
+            key_scale_pool[c] = sb("ksp%d" % c, [P, widths[c]], U8)
             nc.vector.memset(key_scale_pool[c][:].bitcast(I32), 0)
             rows = src[0].rearrange("(quad j) n -> j quad n", j=4)
             for j in range(4):
                 nc.sync.dma_start(out=key_scale_pool[c][scale_row[c] + j:P:32, :].bitcast(I32), in_=rows[j].bitcast(I32))
 
-        def load_values(c, r, at):
-            val_pool[c, r] = sb("vp%d%d" % (c, r), [P, widths[c]], F32, at)
+        def load_values(c, r):
+            val_pool[c, r] = sb("vp%d%d" % (c, r), [P, widths[c]], F32)
             nc.sync.dma_start(out=val_pool[c, r][:], in_=pools[c].rearrange("(m r) t -> r m t", r=PACK)[r])
 
-        slot_w = {}
-
-        def load_slot_weights(c, at=None):
-            slot_w[c] = sb("slot_w%d" % c, [P, PACK], F32, at)
+        def load_slot_weights(c):
+            slot_w[c] = sb("slot_w%d" % c, [P, PACK], F32)
             nc.sync.dma_start(out=slot_w[c][:], in_=(size, rsz)[c].rearrange("o (p t) -> (o p) t", t=PACK))
 
         nc.sync.dma_start(lists[RECENT][:], offs2)
@@ -71,28 +76,23 @@ def tile_attend_two_caches_pl_kernel(tc, query, keys_words, keys_scales, rkey_wo
 
         ident = sb("ident", [P, P], F32)
         zeros = sb("zeros", [P, P], F32)
-        nc.gpsimd.memset(zeros[:, 0:P], 0.0)
-        nc.gpsimd.affine_select(out=ident[:], in_=zeros[:, 0:P], compare_op=ALU.not_equal, fill=1.0, base=0,
+        nc.gpsimd.memset(zeros[:], 0.0)
+        nc.gpsimd.affine_select(out=ident[:], in_=zeros[:], compare_op=ALU.not_equal, fill=1.0, base=0,
                                 pattern=[[-1, P]], channel_multiplier=1)
 
         q_raw = sb("q_raw", [P, PACK, Q], F32)
         nc.sync.dma_start(out=q_raw[:], in_=query.rearrange("(p j) q -> p j q", j=PACK))
-        load_values(RECENT, 0, None)
+        load_values(RECENT, 0)
         nc.sync.dma_start(lists[LONG][:], offs)
         load_scales(LONG, keys_scales)
-        warm = sb("warm", [P, 49 * KIB // 4], F32, at=10)
-        nc.vector.memset(warm[:, 0:1], 0.0)
-        nc.scalar.activation(out=warm[:, 1:2], in_=warm[:, 0:1], func=ACT.Exp)
-        key_word_pool[LONG] = sb("kwp0", [P, T], U16, at=11)
+        key_word_pool[LONG] = sb("kwp0", [P, T], U16)
         nc.sync.dma_start(out=key_word_pool[LONG][:].bitcast(I32), in_=keys_words[0].bitcast(I32))
-        load_values(RECENT, 1, at=15)
-        load_slot_weights(RECENT, at=10.5)
-        load_values(LONG, 0, at=27)
-        load_values(RECENT, 2, at=19)
-        load_values(LONG, 1, at=35)
-        load_values(RECENT, 3, at=23)
-        load_values(LONG, 2, at=43)
-        load_values(LONG, 3, at=51)
+        load_values(RECENT, 1)
+        load_slot_weights(RECENT)
+        load_values(RECENT, 2)
+        load_values(RECENT, 3)
+        for r in range(PACK):
+            load_values(LONG, r)
 
         key_scales = [sb("ks0", [P, SLOTS], U8), sb("ks1", [P, SLOTS], U8)]
         key_words = [sb("kw0", [P, SLOTS], U16), sb("kw1", [P, SLOTS], U32)]
@@ -111,7 +111,8 @@ def tile_attend_two_caches_pl_kernel(tc, query, keys_words, keys_scales, rkey_wo
 
         fmts = (FP4X4, FP8X4)
         scores = {}
-        for c in (RECENT, LONG):
+
+        def score(c):
             for h in range(HALVES):
                 scores[c, h] = bank("score%d%d" % (c, h), [P, SLOTS], 2 * (1 - c) + h)
                 nc.tensor.matmul_mx(out=scores[c, h][:],
@@ -120,156 +121,159 @@ def tile_attend_two_caches_pl_kernel(tc, query, keys_words, keys_scales, rkey_wo
                                     rhs=key_words[c][:].bitcast(fmts[c]), rhs_scale=key_scales[c][scale_row[c]:P, :],
                                     start=True, stop=True)
 
-        casts = {}
+        picked, grouped, v_codes, v_scales = {}, {}, {}, {}
 
-        def cast(r, on_vector=False, at=None):
-            casts[r] = sb("cast%d" % r, [P, U], BF16, at)
-            if on_vector:
-                nc.vector.tensor_copy(out=casts[r][:], in_=val_pool[RECENT, r][:])
+        def gather(engine, c, r, first=0, count=SLOTS, on=None, skip=0):
+            if first == 0:
+                picked[c, r] = sb("picked%d%d" % (c, r), [P, SLOTS], BF16, on, skip)
+            dst = picked[c, r][:, first:first + count]
+            src = val_pool[c, r][:].indirect(lists[c][:, first // 16:(first + count) // 16])
+            if engine == "scalar":
+                nc.scalar.activation(out=dst, in_=src, func=ACT.Copy)
             else:
-                nc.scalar.activation(out=casts[r][:], in_=val_pool[RECENT, r][:], func=ACT.Copy)
+                nc.vector.tensor_copy(dst, src)
 
-        def dealt(ap):
-            return ap.rearrange("p (u b i) -> p b u i", u=2, i=16)
-
-        def turn(src_bf, dst):
-            words = src_bf.bitcast(F32)
+        def turn_values(c, r, dst):
+            words = picked[c, r][:].bitcast(F32)
             for u in range(2):
-                nc.tensor.transpose(dst[:, u, :], words[:, u * P:(u + 1) * P], ident[:])
+                nc.tensor.transpose(dst[:, u, :], words[:, u:2 * P:2], ident[:])
 
-        def pick_and_turn(c, r, dst, at=None):
-            picked = sb("picked%d%d" % (c, r), [P, SLOTS], BF16, at)
-            if c == RECENT:
-                nc.scalar.activation(out=dealt(picked[:]), in_=casts[r][:].indirect(lists[c][:]), func=ACT.Copy)
+        def copy_out(engine, dst, src):
+            if engine == "scalar":
+                nc.scalar.copy(out=dst, in_=src)
             else:
-                nc.vector.tensor_copy(dealt(picked[:]), val_pool[c, r][:].indirect(lists[c][:]))
-            turn(picked[:], dst)
-            return picked
+                nc.vector.tensor_copy(out=dst, in_=src)
 
-        groups = (((RECENT, 0),), ((RECENT, 1), (LONG, 0)), ((RECENT, 2), (LONG, 1)), ((RECENT, 3), (LONG, 2)),
-                  ((LONG, 3),))
-        turned, v_grouped, v_codes, v_scales = {}, {}, {}, {}
+        def copy_turned(engine, dst, turned):
+            copy_out(engine, dst, turned[:].rearrange("p k u m -> p k m u"))
 
-        def open_turn(g, number):
-            turned[g] = bank("vturn%d" % g, [P, len(groups[g]), 2, P], number)
-
-        def copy_out(g, at=None):
-            v_grouped[g] = sb("vg%d" % g, [P, len(groups[g]), P, 2], F32, at)
-            nc.scalar.copy(out=v_grouped[g][:], in_=turned[g][:].rearrange("p k u m -> p k m u"))
-
-        def quantize_values(g, at=None):
-            n = len(groups[g])
-            codes = sb("vc%d" % g, [P, n * P], U32, at)
-            scales = sb("vs%d" % g, [P, n * P], U8)
+        def quantize_values(name, parts, src, on=None, skip=0):
+            n = len(parts)
+            codes = sb("vc" + name, [P, n * P], U32, on, skip)
+            scales = sb("vs" + name, [P, n * P], U8)
             nc.vector.quantize_mx(out=codes[:].bitcast(FP8X4), scales=scales[:],
-                                  in_=v_grouped[g][:].rearrange("p k m u -> p (k m u)").bitcast(BF16))
-            for k, cr in enumerate(groups[g]):
+                                  in_=src.rearrange("p k m u -> p (k m u)").bitcast(BF16))
+            for k, cr in enumerate(parts):
                 v_codes[cr] = codes[:, k * P:(k + 1) * P]
                 v_scales[cr] = scales[:, k * P:(k + 1) * P]
 
-        cast(0)
-        open_turn(0, 6)
-        pick_and_turn(RECENT, 0, turned[0][:, 0])
-        cast(1, at=74)
-        copy_out(0, at=15)
-        open_turn(1, 7)
-        pick_and_turn(RECENT, 1, turned[1][:, 0])
+        def one_part(c, r, number, copier="scalar"):
+            turned = bank("turn%d%d" % (c, r), [P, 1, 2, P], number)
+            turn_values(c, r, turned[:, 0])
+            grouped[c, r] = sb("vg%d%d" % (c, r), [P, 1, P, 2], F32)
+            copy_turned(copier, grouped[c, r][:], turned)
 
-        neg_first = [sb("neg_first0", [P, 1], F32, at=11), sb("neg_first1", [P, 1], F32, at=12)]
+        score(RECENT)
+        gather("scalar", RECENT, 0)
+        recent = sb("vg_recent", [P, 3, P, 2], F32)
+        turned0 = bank("turn0", [P, 1, 2, P], 2)
+        turn_values(RECENT, 0, turned0[:, 0])
+        copy_turned("scalar", recent[:, 0:1], turned0)
+        score(LONG)
+        gather("scalar", RECENT, 1)
+        gather("scalar", RECENT, 2)
+        turned12 = bank("turn12", [P, 2, 2, P], 7)
+        turn_values(RECENT, 1, turned12[:, 0])
+        turn_values(RECENT, 2, turned12[:, 1])
+
+        neg_first = [sb("neg_first%d" % h, [P, 1], F32, "kwp0", 64 * h) for h in range(HALVES)]
         neg_max = sb("neg_max", [P, HALVES], F32)
-        row_sum = [sb("row_sum0", [P, 1], F32, at=74), sb("row_sum1", [P, 1], F32, at=74.25)]
-        neg_scores = [sb("neg_scores0", [P, 2, SLOTS], F32, at=60), sb("neg_scores1", [P, 2, SLOTS], F32, at=64)]
-        probs = [sb("probs0", [P, 2, SLOTS], F32, at=0), sb("probs1", [P, 2, SLOTS], F32, at=4)]
+        row_sum = [sb("row_sum%d" % h, [P, 1], F32, "vp12", 64 * h) for h in range(HALVES)]
+        neg_scores = [sb("neg_scores%d" % h, [P, 2, SLOTS], F32) for h in range(HALVES)]
+        probs = [sb("probs0", [P, 2, SLOTS], F32), sb("probs1", [P, 2, SLOTS], F32)]
+
+        def negate(c, h, start, least):
+            nc.vector.tensor_scalar(out=neg_scores[h][:, c, :].rearrange("q (u p e) -> q u p e", u=2, e=2),
+                                    in0=scores[c, h][:].rearrange("q (p u e) -> q u p e", u=2, e=2),
+                                    scalar1=-1.0, scalar2=start, op0=ALU.mult, op1=ALU.min, accum_out=least)
+
         for h in range(HALVES):
-            nc.vector.tensor_scalar(out=dealt(neg_scores[h][:, RECENT, :]), in0=scores[RECENT, h][:].rearrange("p (b u i) -> p b u i", u=2, i=16), scalar1=-1.0,
-                                    scalar2=None, op0=ALU.mult, op1=ALU.min, accum_out=neg_first[h][:])
+            negate(RECENT, h, None, neg_first[h][:])
         for h in range(HALVES):
-            nc.vector.tensor_scalar(out=dealt(neg_scores[h][:, LONG, :]), in0=scores[LONG, h][:].rearrange("p (b u i) -> p b u i", u=2, i=16), scalar1=-1.0,
-                                    scalar2=neg_first[h][:], op0=ALU.mult, op1=ALU.min,
-                                    accum_out=neg_max[:, h:h + 1])
+            negate(LONG, h, neg_first[h][:], neg_max[:, h:h + 1])
             nc.scalar.activation(out=probs[h][:], in_=neg_scores[h][:], func=ACT.Exp,
                                  bias=neg_max[:, h:h + 1], scale=-1.0, accum_out=row_sum[h][:])
         spread = {}
-        for c in (RECENT, LONG):
-            spread[c] = bank("spread%d" % c, [P, SLOTS], 4 + c)
+        for c in (LONG, RECENT):
+            spread[c] = bank("spread%d" % c, [P, 2, P, 2], 4 + c)
             for t in range(PACK):
-                nc.tensor.transpose(spread[c][:].rearrange("p (u b j t) -> p t b u j", u=2, j=4, t=PACK)[:, t], slot_w[c][:, t:t + 1].to_broadcast([P, P]), ident[:])
+                nc.tensor.transpose(spread[c][:, t // 2, :, t % 2], slot_w[c][:, t:t + 1].to_broadcast([P, P]), ident[:])
 
-        pick_and_turn(LONG, 0, turned[1][:, 1], at=11)
-        cast(2, on_vector=True, at=12)
+        copy_turned("vector", recent[:, 1:3], turned12)
         inv_sum = [sb("inv_sum%d" % h, [P, 1], F32) for h in range(HALVES)]
         nc.vector.reciprocal(out=inv_sum[0][:], in_=row_sum[0][:])
-        quantize_values(0, at=60)
+        quantize_values("a", [(RECENT, r) for r in range(3)], recent[:], "neg_scores0")
 
         w_turned = [bank("wturn%d" % h, [P, 2, 2, P], h) for h in range(HALVES)]
-        w_grouped = sb("wg", [P, 2, HALVES, P, 2], F32, at=21)
 
-        def weigh(h, c, at=None):
-            weights = sb("weights%d%d" % (c, h), [P, SLOTS], BF16, at)
+        def weigh(h, c, on=None, skip=0):
+            weights = sb("weights%d%d" % (c, h), [P, SLOTS], BF16, on, skip)
             nc.vector.scalar_tensor_tensor(out=weights[:], in0=probs[h][:, c, :], scalar=inv_sum[h][:],
-                                           in1=spread[c][:], op0=ALU.mult, op1=ALU.mult)
-            turn(weights[:], w_turned[h][:, c])
-            return weights
+                                           in1=spread[c][:].rearrange("q u p e -> q (u p e)"),
+                                           op0=ALU.mult, op1=ALU.mult)
+            words = weights[:].bitcast(F32)
+            for u in range(2):
+                nc.tensor.transpose(w_turned[h][:, c, u, :], words[:, u * P:(u + 1) * P], ident[:])
 
-        def copy_weights(h):
-            nc.scalar.copy(out=w_grouped[:, :, h], in_=w_turned[h][:].rearrange("p c u q -> p c q u"))
-
-        w0b = weigh(0, RECENT, at=72)
+        weigh(0, RECENT)
         nc.vector.reciprocal(out=inv_sum[1][:], in_=row_sum[1][:])
-        weigh(0, LONG, at=68)
-        copy_out(1, at=64)
-        open_turn(2, 2)
-        pick_and_turn(RECENT, 2, turned[2][:, 0], at=72)
+        weigh(0, LONG)
         weigh(1, RECENT)
-        quantize_values(1, at=1)
-        weigh(1, LONG, at=70)
-        cast(3, at=68)
-        copy_weights(0)
-        copy_weights(1)
-        idle = bank("idle", [P, SLOTS], 1)
-        for first in (True, False):
-            nc.tensor.matmul_mx(out=idle[:], lhsT=q_codes[:, 0:P].bitcast(FP8X4), lhsT_scale=q_scales[:, 0:P],
-                                rhs=key_words[RECENT][:].bitcast(FP8X4),
-                                rhs_scale=key_scales[RECENT][scale_row[RECENT]:P, :], start=first, stop=not first)
-        pick_and_turn(LONG, 1, turned[2][:, 1], at=0)
-        open_turn(3, 3)
-        pick_and_turn(RECENT, 3, turned[3][:, 0], at=70)
-        pick_and_turn(LONG, 2, turned[3][:, 1], at=5)
-        w_codes = sb("wc", [P, 2, Q], U32, at=43)
+        gather("scalar", LONG, 0)
+        weigh(1, LONG, "vp00", 4096)
+        gather("vector", RECENT, 3, on="vp00", skip=5120)
+        w_grouped = sb("wg", [P, 2, HALVES, P, 2], F32, "vp00")
+        nc.scalar.copy(out=w_grouped[:, :, 0], in_=w_turned[0][:].rearrange("p c u q -> p c q u"))
+        one_part(LONG, 0, 6)
+        nc.scalar.copy(out=w_grouped[:, :, 1], in_=w_turned[1][:].rearrange("p c u q -> p c q u"))
+        w_codes = sb("wc", [P, 2, Q], U32)
         w_scales = sb("ws", [P, 2, Q], U8)
         nc.vector.quantize_mx(out=w_codes[:].rearrange("p c q -> p (c q)").bitcast(FP8X4),
                               scales=w_scales[:].rearrange("p c q -> p (c q)"),
                               in_=w_grouped[:].rearrange("p c h q u -> p (c h q u)").bitcast(BF16))
-        copy_out(2, at=25)
-        copy_out(3)
+        quantize_values("b", [(LONG, 0)], grouped[LONG, 0][:])
+        gather("scalar", LONG, 1)
+        turned31 = bank("turn31", [P, 2, 2, P], 5)
+        turn_values(RECENT, 3, turned31[:, 0])
+        turn_values(LONG, 1, turned31[:, 1])
+        pair = sb("vg_pair", [P, 2, P, 2], F32)
+        copy_turned("scalar", pair[:], turned31)
+        gather("vector", LONG, 2)
+        turned2 = bank("turn2", [P, 1, 2, P], 2)
+        turn_values(LONG, 2, turned2[:, 0])
 
-        early = bank("early", [P, 2, Q], 4)
-        third = bank("third", [P, Q], 5)
-        last = [bank("last%d" % h, [P, P], h) for h in range(HALVES)]
-        out_sb = sb("out_sb", [P, PACK, Q], F32)
+        early = bank("early", [P, 2, Q], 3)
+        third = bank("third", [P, Q], 4)
+        last = [bank("last0", [P, P], 0), bank("last1", [P, P], 1)]
         out_rows = out_0.rearrange("(p r) q -> p r q", r=PACK)
         halves = [slice(h * P, (h + 1) * P) for h in range(HALVES)]
 
-        def multiply(dst, c, r, start, columns=slice(0, Q)):
+        def multiply(dst, c, r, start, stop, columns=slice(0, Q)):
             nc.tensor.matmul_mx(out=dst, lhsT=v_codes[c, r].bitcast(FP8X4), lhsT_scale=v_scales[c, r],
                                 rhs=w_codes[:, c, columns].bitcast(FP8X4), rhs_scale=w_scales[:, c, columns],
-                                start=start, stop=not start)
+                                start=start, stop=stop)
 
-        multiply(early[:, 0, :], RECENT, 0, True)
-        multiply(early[:, 0, :], LONG, 0, False)
-        open_turn(4, 6)
-        pk3 = pick_and_turn(LONG, 3, turned[4][:, 0])
-        quantize_values(2, at=51)
-        quantize_values(3, at=52)
-        copy_out(4)
-        for r, dst in ((1, early[:, 1, :]), (2, third[:])):
-            multiply(dst, LONG, r, True)
-            multiply(dst, RECENT, r, False)
+        multiply(early[:, 0, :], RECENT, 0, True, False)
+        multiply(early[:, 1, :], RECENT, 1, False, False)
+        multiply(third[:], RECENT, 2, True, False)
+        multiply(early[:, 0, :], LONG, 0, False, False)
+
+        gather("vector", LONG, 3, 0, SHARE)
+        gather("scalar", LONG, 3, SHARE, SLOTS - SHARE)
+        grouped2 = sb("vg_third", [P, 1, P, 2], F32, "vp03")
+        copy_turned("scalar", grouped2[:], turned2)
+        quantize_values("c", [(RECENT, 3), (LONG, 1)], pair[:], "vp03", 1024)
+        one_part(LONG, 3, 7)
+        multiply(early[:, 1, :], LONG, 1, False, True)
         for h in range(HALVES):
-            multiply(last[h][:], RECENT, 3, True, halves[h])
-        quantize_values(4)
+            multiply(last[h][:], RECENT, 3, True, False, halves[h])
+        quantize_values("d", [(LONG, 2)], grouped2[:])
+        multiply(third[:], LONG, 2, False, True)
+        quantize_values("e", [(LONG, 3)], grouped[LONG, 3][:])
         for h in range(HALVES):
-            multiply(last[h][:], LONG, 3, False, halves[h])
+            multiply(last[h][:], LONG, 3, False, True, halves[h])
+
+        out_sb = sb("out_sb", [P, PACK, Q], F32)
         nc.scalar.copy(out=out_sb[:, 0:2, :], in_=early[:])
         nc.sync.dma_start(out=out_rows[:, 0:2, :], in_=out_sb[:, 0:2, :])
         nc.vector.tensor_copy(out=out_sb[:, 2, :], in_=third[:])
@@ -285,7 +289,7 @@ def tile_attend_two_caches_pl_kernel(tc, query, keys_words, keys_scales, rkey_wo
         nc.scalar.copy(out=o_bf[1][:].rearrange("p (c i) r -> p c r i", i=4),
                        in_=out_sb[:, :, P:Q].rearrange("p r (c i) -> p c r i", i=4))
         for h in range(HALVES):
-            nc.vector.quantize_mx(out=o_codes[:, h * P:(h + 1) * P].bitcast(FP8X4), scales=o_scales[:, h * P:(h + 1) * P],
+            nc.vector.quantize_mx(out=o_codes[:, halves[h]].bitcast(FP8X4), scales=o_scales[:, halves[h]],
                                   in_=o_bf[h][:].rearrange("p q r -> p (q r)"))
         nc.sync.dma_start(out=out_1[0].rearrange("p c t -> p (c t)").bitcast(I32), in_=o_codes[:].bitcast(I32))
         for quad in range(4):

@@ -20,7 +20,7 @@ HALVES = Q // P
 FLOPS = 2 * 2 * D * Q * SLOTS + 2 * 2 * SLOTS * E * Q
 BYTES_OF = {F32: 4, U32: 4, BF16: 2, U16: 2, U8: 1}
 LONG, RECENT = 0, 1
-SHARE = 352
+SHARE = 256
 
 
 def tile_attend_two_caches_pl_kernel(tc, query, keys_words, keys_scales, rkey_words, rkey_scales,
@@ -157,10 +157,10 @@ def tile_attend_two_caches_pl_kernel(tc, query, keys_words, keys_scales, rkey_wo
                 v_codes[cr] = codes[:, k * P:(k + 1) * P]
                 v_scales[cr] = scales[:, k * P:(k + 1) * P]
 
-        def one_part(c, r, number, copier="scalar"):
+        def one_part(c, r, number, copier="scalar", on=None):
             turned = bank("turn%d%d" % (c, r), [P, 1, 2, P], number)
             turn_values(c, r, turned[:, 0])
-            grouped[c, r] = sb("vg%d%d" % (c, r), [P, 1, P, 2], F32)
+            grouped[c, r] = sb("vg%d%d" % (c, r), [P, 1, P, 2], F32, on)
             copy_turned(copier, grouped[c, r][:], turned)
 
         score(RECENT)
@@ -219,32 +219,34 @@ def tile_attend_two_caches_pl_kernel(tc, query, keys_words, keys_scales, rkey_wo
         nc.vector.reciprocal(out=inv_sum[1][:], in_=row_sum[1][:])
         weigh(0, LONG)
         weigh(1, RECENT)
+        weigh(1, LONG)
+        gather("vector", RECENT, 3, on="row_sum1")
         gather("scalar", LONG, 0)
-        weigh(1, LONG, "vp00", 4096)
-        gather("vector", RECENT, 3, on="vp00", skip=5120)
-        w_grouped = sb("wg", [P, 2, HALVES, P, 2], F32, "vp00")
-        nc.scalar.copy(out=w_grouped[:, :, 0], in_=w_turned[0][:].rearrange("p c u q -> p c q u"))
-        one_part(LONG, 0, 6)
-        nc.scalar.copy(out=w_grouped[:, :, 1], in_=w_turned[1][:].rearrange("p c u q -> p c q u"))
+        gather("scalar", LONG, 1)
+        turned01 = bank("turn01", [P, 2, 2, P], 4)
+        turn_values(LONG, 0, turned01[:, 0])
+        turn_values(LONG, 1, turned01[:, 1])
+        w_grouped = sb("wg", [P, 2, HALVES, P, 2], F32, "vp01")
+        for h in range(HALVES):
+            nc.scalar.copy(out=w_grouped[:, :, h], in_=w_turned[h][:].rearrange("p c u q -> p c q u"))
+        turned3 = bank("turn3", [P, 1, 2, P], 0)
+        turn_values(RECENT, 3, turned3[:, 0])
+        pair = sb("vg_pair", [P, 2, P, 2], F32)
+        copy_turned("vector", pair[:], turned01)
         w_codes = sb("wc", [P, 2, Q], U32)
         w_scales = sb("ws", [P, 2, Q], U8)
         nc.vector.quantize_mx(out=w_codes[:].rearrange("p c q -> p (c q)").bitcast(FP8X4),
                               scales=w_scales[:].rearrange("p c q -> p (c q)"),
                               in_=w_grouped[:].rearrange("p c h q u -> p (c h q u)").bitcast(BF16))
-        quantize_values("b", [(LONG, 0)], grouped[LONG, 0][:])
-        gather("scalar", LONG, 1)
-        turned31 = bank("turn31", [P, 2, 2, P], 5)
-        turn_values(RECENT, 3, turned31[:, 0])
-        turn_values(LONG, 1, turned31[:, 1])
-        pair = sb("vg_pair", [P, 2, P, 2], F32)
-        copy_turned("scalar", pair[:], turned31)
-        gather("vector", LONG, 2)
+        grouped3 = sb("vg_recent3", [P, 1, P, 2], F32, "wg")
+        copy_turned("vector", grouped3[:], turned3)
+        gather("scalar", LONG, 2)
         turned2 = bank("turn2", [P, 1, 2, P], 2)
         turn_values(LONG, 2, turned2[:, 0])
 
         early = bank("early", [P, 2, Q], 3)
-        third = bank("third", [P, Q], 4)
-        last = [bank("last0", [P, P], 0), bank("last1", [P, P], 1)]
+        third = bank("third", [P, Q], 5)
+        last = [bank("last0", [P, P], 6), bank("last1", [P, P], 1)]
         out_rows = out_0.rearrange("(p r) q -> p r q", r=PACK)
         halves = [slice(h * P, (h + 1) * P) for h in range(HALVES)]
 
@@ -256,14 +258,15 @@ def tile_attend_two_caches_pl_kernel(tc, query, keys_words, keys_scales, rkey_wo
         multiply(early[:, 0, :], RECENT, 0, True, False)
         multiply(early[:, 1, :], RECENT, 1, False, False)
         multiply(third[:], RECENT, 2, True, False)
-        multiply(early[:, 0, :], LONG, 0, False, False)
 
         gather("vector", LONG, 3, 0, SHARE)
         gather("scalar", LONG, 3, SHARE, SLOTS - SHARE)
         grouped2 = sb("vg_third", [P, 1, P, 2], F32, "vp03")
         copy_turned("scalar", grouped2[:], turned2)
-        quantize_values("c", [(RECENT, 3), (LONG, 1)], pair[:], "vp03", 1024)
+        quantize_values("b", [(LONG, 0), (LONG, 1)], pair[:], "vp03", 1024)
+        quantize_values("c", [(RECENT, 3)], grouped3[:], "vp03", 2048)
         one_part(LONG, 3, 7)
+        multiply(early[:, 0, :], LONG, 0, False, False)
         multiply(early[:, 1, :], LONG, 1, False, True)
         for h in range(HALVES):
             multiply(last[h][:], RECENT, 3, True, False, halves[h])

@@ -20,7 +20,7 @@ HALVES = Q // P
 FLOPS = 2 * 2 * D * Q * SLOTS + 2 * 2 * SLOTS * E * Q
 BYTES_OF = {F32: 4, U32: 4, BF16: 2, U16: 2, U8: 1}
 LONG, RECENT = 0, 1
-SHARE = 256
+SHARE = 320
 
 
 def tile_attend_two_caches_pl_kernel(tc, query, keys_words, keys_scales, rkey_words, rkey_scales,
@@ -50,7 +50,7 @@ def tile_attend_two_caches_pl_kernel(tc, query, keys_words, keys_scales, rkey_wo
         lists = [keep.tile([P, SLOTS // 16], U16, name="list0"), keep.tile([P, SLOTS // 16], U16, name="list1")]
         pools = (vals, rval)
         widths = (T, U)
-        val_pool, key_scale_pool, key_word_pool, slot_w = {}, {}, {}, {}
+        val_pool, key_scale_pool, key_word_pool = {}, {}, {}
 
         def load_scales(c, src):
             key_scale_pool[c] = sb("ksp%d" % c, [P, widths[c]], U8)
@@ -63,16 +63,18 @@ def tile_attend_two_caches_pl_kernel(tc, query, keys_words, keys_scales, rkey_wo
             val_pool[c, r] = sb("vp%d%d" % (c, r), [P, widths[c]], F32)
             nc.sync.dma_start(out=val_pool[c, r][:], in_=pools[c].rearrange("(m r) t -> r m t", r=PACK)[r])
 
-        def load_slot_weights(c):
-            slot_w[c] = sb("slot_w%d" % c, [P, PACK], F32)
-            nc.sync.dma_start(out=slot_w[c][:], in_=(size, rsz)[c].rearrange("o (p t) -> (o p) t", t=PACK))
+        size_rows = sb("size_rows", [P, P], F32)
 
-        nc.sync.dma_start(lists[RECENT][:], offs2)
-        load_slot_weights(LONG)
+        def load_sizes(c):
+            nc.sync.dma_start(out=size_rows[PACK * c:PACK * c + PACK, :],
+                              in_=(size, rsz)[c].rearrange("o (j s) -> (o j) s", j=PACK))
+
         key_word_pool[RECENT] = sb("kwp1", [P, U], U32)
         nc.sync.dma_start(out=key_word_pool[RECENT][:].bitcast(I32),
                           in_=rkey_words[0].rearrange("p n t -> p (n t)").bitcast(I32))
+        nc.sync.dma_start(lists[RECENT][:], offs2)
         load_scales(RECENT, rkey_scales)
+        nc.vector.memset(size_rows[:], 0.0)
 
         ident = sb("ident", [P, P], F32)
         zeros = sb("zeros", [P, P], F32)
@@ -88,7 +90,8 @@ def tile_attend_two_caches_pl_kernel(tc, query, keys_words, keys_scales, rkey_wo
         key_word_pool[LONG] = sb("kwp0", [P, T], U16)
         nc.sync.dma_start(out=key_word_pool[LONG][:].bitcast(I32), in_=keys_words[0].bitcast(I32))
         load_values(RECENT, 1)
-        load_slot_weights(RECENT)
+        load_sizes(LONG)
+        load_sizes(RECENT)
         load_values(RECENT, 2)
         load_values(RECENT, 3)
         for r in range(PACK):
@@ -171,7 +174,11 @@ def tile_attend_two_caches_pl_kernel(tc, query, keys_words, keys_scales, rkey_wo
         copy_turned("scalar", recent[:, 0:1], turned0)
         score(LONG)
         gather("scalar", RECENT, 1)
+        size_turned = bank("size_turned", [P, P], 6)
+        nc.tensor.transpose(size_turned[:], size_rows[:], ident[:])
         gather("scalar", RECENT, 2)
+        size_cols = sb("size_cols", [P, 2 * PACK], F32, "vp12", 128)
+        nc.scalar.copy(out=size_cols[:], in_=size_turned[:, 0:2 * PACK])
         turned12 = bank("turn12", [P, 2, 2, P], 7)
         turn_values(RECENT, 1, turned12[:, 0])
         turn_values(RECENT, 2, turned12[:, 1])
@@ -194,10 +201,11 @@ def tile_attend_two_caches_pl_kernel(tc, query, keys_words, keys_scales, rkey_wo
             nc.scalar.activation(out=probs[h][:], in_=neg_scores[h][:], func=ACT.Exp,
                                  bias=neg_max[:, h:h + 1], scale=-1.0, accum_out=row_sum[h][:])
         spread = {}
-        for c in (LONG, RECENT):
+        for c in (RECENT, LONG):
             spread[c] = bank("spread%d" % c, [P, 2, P, 2], 4 + c)
-            for t in range(PACK):
-                nc.tensor.transpose(spread[c][:, t // 2, :, t % 2], slot_w[c][:, t:t + 1].to_broadcast([P, P]), ident[:])
+            for j in range(PACK):
+                nc.tensor.transpose(spread[c][:, :, 32 * j:32 * j + 32, :].rearrange("q u p e -> q p u e"),
+                                    size_cols[:, PACK * c + j:PACK * c + j + 1].to_broadcast([P, P]), ident[:])
 
         copy_turned("vector", recent[:, 1:3], turned12)
         inv_sum = [sb("inv_sum%d" % h, [P, 1], F32) for h in range(HALVES)]
@@ -227,8 +235,8 @@ def tile_attend_two_caches_pl_kernel(tc, query, keys_words, keys_scales, rkey_wo
         turn_values(LONG, 0, turned01[:, 0])
         turn_values(LONG, 1, turned01[:, 1])
         w_grouped = sb("wg", [P, 2, HALVES, P, 2], F32, "vp01")
-        for h in range(HALVES):
-            nc.scalar.copy(out=w_grouped[:, :, h], in_=w_turned[h][:].rearrange("p c u q -> p c q u"))
+        for h, engine in enumerate(("scalar", "vector")):
+            copy_out(engine, w_grouped[:, :, h], w_turned[h][:].rearrange("p c u q -> p c q u"))
         turned3 = bank("turn3", [P, 1, 2, P], 0)
         turn_values(RECENT, 3, turned3[:, 0])
         pair = sb("vg_pair", [P, 2, P, 2], F32)
@@ -280,9 +288,10 @@ def tile_attend_two_caches_pl_kernel(tc, query, keys_words, keys_scales, rkey_wo
         nc.scalar.copy(out=out_sb[:, 0:2, :], in_=early[:])
         nc.sync.dma_start(out=out_rows[:, 0:2, :], in_=out_sb[:, 0:2, :])
         nc.vector.tensor_copy(out=out_sb[:, 2, :], in_=third[:])
+        nc.sync.dma_start(out=out_rows[:, 2, :], in_=out_sb[:, 2, :])
         nc.vector.tensor_copy(out=out_sb[:, 3, 0:P], in_=last[0][:])
         nc.scalar.copy(out=out_sb[:, 3, P:Q], in_=last[1][:])
-        nc.sync.dma_start(out=out_rows[:, 2:4, :], in_=out_sb[:, 2:4, :])
+        nc.sync.dma_start(out=out_rows[:, 3, :], in_=out_sb[:, 3, :])
 
         o_codes = sb("o_codes", [P, Q], U32)
         o_scales = sb("o_scales", [P, Q], U8)

@@ -241,6 +241,11 @@ def tile_attend_two_caches_pl_kernel(tc, query, keys_words, keys_scales, rkey_wo
         turn_values(RECENT, 3, turned3[:, 0])
         pair = sb("vg_pair", [P, 2, P, 2], F32)
         copy_turned("vector", pair[:], turned01)
+        warm = bank("warm", [P, Q + P], 1)
+        for first, count in ((0, Q), (Q, P)):
+            nc.tensor.matmul_mx(out=warm[:, first:first + count], lhsT=q_codes[:, 0:P].bitcast(FP8X4),
+                                lhsT_scale=q_scales[:, 0:P], rhs=q_codes[:, 0:count].bitcast(FP8X4),
+                                rhs_scale=q_scales[:, 0:count], start=True, stop=True)
         w_codes = sb("wc", [P, 2, Q], U32)
         w_scales = sb("ws", [P, 2, Q], U8)
         nc.vector.quantize_mx(out=w_codes[:].rearrange("p c q -> p (c q)").bitcast(FP8X4),

@@ -20,7 +20,8 @@ HALVES = Q // P
 FLOPS = 2 * 2 * D * Q * SLOTS + 2 * 2 * SLOTS * E * Q
 BYTES_OF = {F32: 4, U32: 4, BF16: 2, U16: 2, U8: 1}
 LONG, RECENT = 0, 1
-SHARE = 320
+SHARE = 288
+ROUND_SHARE = 160
 
 
 def tile_attend_two_caches_pl_kernel(tc, query, keys_words, keys_scales, rkey_words, rkey_scales,
@@ -281,10 +282,10 @@ def tile_attend_two_caches_pl_kernel(tc, query, keys_words, keys_scales, rkey_wo
         one_part(LONG, 3, 7)
         multiply(early[:, 0, :], LONG, 0, False, False)
         multiply(early[:, 1, :], LONG, 1, False, True)
-        for h in range(HALVES):
-            multiply(last[h][:], RECENT, 3, True, False, halves[h])
         quantize_values("d", [(LONG, 2)], grouped2[:])
         multiply(third[:], LONG, 2, False, True)
+        for h in range(HALVES):
+            multiply(last[h][:], RECENT, 3, True, False, halves[h])
         quantize_values("e", [(LONG, 3)], grouped[LONG, 3][:])
         for h in range(HALVES):
             multiply(last[h][:], LONG, 3, False, True, halves[h])
@@ -293,23 +294,22 @@ def tile_attend_two_caches_pl_kernel(tc, query, keys_words, keys_scales, rkey_wo
         nc.scalar.copy(out=out_sb[:, 0:2, :], in_=early[:])
         nc.sync.dma_start(out=out_rows[:, 0:2, :], in_=out_sb[:, 0:2, :])
         nc.vector.tensor_copy(out=out_sb[:, 2, :], in_=third[:])
-        nc.sync.dma_start(out=out_rows[:, 2, :], in_=out_sb[:, 2, :])
         nc.vector.tensor_copy(out=out_sb[:, 3, 0:P], in_=last[0][:])
         nc.scalar.copy(out=out_sb[:, 3, P:Q], in_=last[1][:])
-        nc.sync.dma_start(out=out_rows[:, 3, :], in_=out_sb[:, 3, :])
+        nc.sync.dma_start(out=out_rows[:, 2:4, :], in_=out_sb[:, 2:4, :])
 
         o_codes = sb("o_codes", [P, Q], U32)
         o_scales = sb("o_scales", [P, Q], U8)
-        o_bf = [sb("o_bf%d" % h, [P, P, PACK], BF16) for h in range(HALVES)]
-        nc.vector.tensor_copy(out=o_bf[0][:].rearrange("p (c i) r -> p c r i", i=4),
-                              in_=out_sb[:, :, 0:P].rearrange("p r (c i) -> p c r i", i=4))
-        nc.scalar.copy(out=o_bf[1][:].rearrange("p (c i) r -> p c r i", i=4),
-                       in_=out_sb[:, :, P:Q].rearrange("p r (c i) -> p c r i", i=4))
+        o_bf = sb("o_bf", [P, Q, PACK], BF16)
+        for engine, first, stop in (("vector", 0, P), ("scalar", ROUND_SHARE, Q), ("vector", P, ROUND_SHARE)):
+            copy_out(engine, o_bf[:, first:stop, :].rearrange("p (c i) r -> p c r i", i=4),
+                     out_sb[:, :, first:stop].rearrange("p r (c i) -> p c r i", i=4))
+        out_words = out_1[0].rearrange("p c t -> p (c t)").bitcast(I32)
         for h in range(HALVES):
             nc.vector.quantize_mx(out=o_codes[:, halves[h]].bitcast(FP8X4), scales=o_scales[:, halves[h]],
-                                  in_=o_bf[h][:].rearrange("p q r -> p (q r)"))
-        nc.sync.dma_start(out=out_1[0].rearrange("p c t -> p (c t)").bitcast(I32), in_=o_codes[:].bitcast(I32))
+                                  in_=o_bf[:, halves[h], :].rearrange("p q r -> p (q r)"))
+            nc.sync.dma_start(out=out_words[:, halves[h]], in_=o_codes[:, halves[h]].bitcast(I32))
         for quad in range(4):
-            queue = nc.sync if quad < 2 else nc.scalar
+            queue = nc.sync if quad < 1 else nc.scalar
             queue.dma_start(out=out_2[0, 4 * quad:4 * quad + 4, :].bitcast(I32),
                             in_=o_scales[32 * quad:32 * quad + 4, :].bitcast(I32))

@@ -130,7 +130,7 @@ def tile_attend_two_caches_pl_kernel(tc, query, keys_words, keys_scales, rkey_wo
         def gather(engine, c, r, first=0, count=SLOTS, on=None, skip=0):
             if first == 0:
                 picked[c, r] = sb("picked%d%d" % (c, r), [P, SLOTS], BF16, on, skip)
-            dst = picked[c, r][:, first:first + count]
+            dst = picked[c, r][:].rearrange("p (u b k) -> p b u k", u=2, k=16)[:, first // 32:(first + count) // 32]
             src = val_pool[c, r][:].indirect(lists[c][:, first // 16:(first + count) // 16])
             if engine == "scalar":
                 nc.scalar.activation(out=dst, in_=src, func=ACT.Copy)
@@ -140,7 +140,7 @@ def tile_attend_two_caches_pl_kernel(tc, query, keys_words, keys_scales, rkey_wo
         def turn_values(c, r, dst):
             words = picked[c, r][:].bitcast(F32)
             for u in range(2):
-                nc.tensor.transpose(dst[:, u, :], words[:, u:2 * P:2], ident[:])
+                nc.tensor.transpose(dst[:, u, :], words[:, u * P:(u + 1) * P], ident[:])
 
         def copy_out(engine, dst, src):
             if engine == "scalar":
@@ -191,8 +191,8 @@ def tile_attend_two_caches_pl_kernel(tc, query, keys_words, keys_scales, rkey_wo
         probs = [sb("probs0", [P, 2, SLOTS], F32), sb("probs1", [P, 2, SLOTS], F32)]
 
         def negate(c, h, start, least):
-            nc.vector.tensor_scalar(out=neg_scores[h][:, c, :].rearrange("q (u p e) -> q u p e", u=2, e=2),
-                                    in0=scores[c, h][:].rearrange("q (p u e) -> q u p e", u=2, e=2),
+            nc.vector.tensor_scalar(out=neg_scores[h][:, c, :].rearrange("q (u b k) -> q u b k", u=2, k=16),
+                                    in0=scores[c, h][:].rearrange("q (b u k) -> q u b k", u=2, k=16),
                                     scalar1=-1.0, scalar2=start, op0=ALU.mult, op1=ALU.min, accum_out=least)
 
         for h in range(HALVES):
@@ -203,9 +203,9 @@ def tile_attend_two_caches_pl_kernel(tc, query, keys_words, keys_scales, rkey_wo
                                  bias=neg_max[:, h:h + 1], scale=-1.0, accum_out=row_sum[h][:])
         spread = {}
         for c in (RECENT, LONG):
-            spread[c] = bank("spread%d" % c, [P, 2, P, 2], 4 + c)
+            spread[c] = bank("spread%d" % c, [P, 2, 16, 16], 4 + c)
             for j in range(PACK):
-                nc.tensor.transpose(spread[c][:, :, 32 * j:32 * j + 32, :].rearrange("q u p e -> q p u e"),
+                nc.tensor.transpose(spread[c][:, :, 4 * j:4 * j + 4, :].rearrange("q u b k -> q b u k"),
                                     size_cols[:, PACK * c + j:PACK * c + j + 1].to_broadcast([P, P]), ident[:])
 
         copy_turned("vector", recent[:, 1:3], turned12)
@@ -218,7 +218,7 @@ def tile_attend_two_caches_pl_kernel(tc, query, keys_words, keys_scales, rkey_wo
         def weigh(h, c, on=None, skip=0):
             weights = sb("weights%d%d" % (c, h), [P, SLOTS], BF16, on, skip)
             nc.vector.scalar_tensor_tensor(out=weights[:], in0=probs[h][:, c, :], scalar=inv_sum[h][:],
-                                           in1=spread[c][:].rearrange("q u p e -> q (u p e)"),
+                                           in1=spread[c][:].rearrange("q u b k -> q (u b k)"),
                                            op0=ALU.mult, op1=ALU.mult)
             words = weights[:].bitcast(F32)
             for u in range(2):

@@ -242,8 +242,8 @@ def tile_attend_two_caches_pl_kernel(tc, query, keys_words, keys_scales, rkey_wo
         turn_values(RECENT, 3, turned3[:, 0])
         pair = sb("vg_pair", [P, 2, P, 2], F32)
         copy_turned("vector", pair[:], turned01)
-        warm = bank("warm", [P, Q + P], 1)
-        for first, count in ((0, Q), (Q, P)):
+        warm = bank("warm", [P, Q + P], 4)
+        for first, count in ((0, P), (P, Q)):
             nc.tensor.matmul_mx(out=warm[:, first:first + count], lhsT=q_codes[:, 0:P].bitcast(FP8X4),
                                 lhsT_scale=q_scales[:, 0:P], rhs=q_codes[:, 0:count].bitcast(FP8X4),
                                 rhs_scale=q_scales[:, 0:count], start=True, stop=True)
@@ -255,8 +255,6 @@ def tile_attend_two_caches_pl_kernel(tc, query, keys_words, keys_scales, rkey_wo
         grouped3 = sb("vg_recent3", [P, 1, P, 2], F32, "wg")
         copy_turned("vector", grouped3[:], turned3)
         gather("scalar", LONG, 2)
-        turned2 = bank("turn2", [P, 1, 2, P], 2)
-        turn_values(LONG, 2, turned2[:, 0])
 
         early = bank("early", [P, 2, Q], 3)
         third = bank("third", [P, Q], 5)
@@ -272,6 +270,8 @@ def tile_attend_two_caches_pl_kernel(tc, query, keys_words, keys_scales, rkey_wo
         multiply(early[:, 0, :], RECENT, 0, True, False)
         multiply(early[:, 1, :], RECENT, 1, False, False)
         multiply(third[:], RECENT, 2, True, False)
+        turned2 = bank("turn2", [P, 1, 2, P], 0)
+        turn_values(LONG, 2, turned2[:, 0])
 
         gather("vector", LONG, 3, 0, SHARE)
         gather("scalar", LONG, 3, SHARE, SLOTS - SHARE)

@@ -235,24 +235,25 @@ def tile_attend_two_caches_pl_kernel(tc, query, keys_words, keys_scales, rkey_wo
         turned01 = bank("turn01", [P, 2, 2, P], 4)
         turn_values(LONG, 0, turned01[:, 0])
         turn_values(LONG, 1, turned01[:, 1])
-        w_grouped = sb("wg", [P, 2, HALVES, P, 2], F32, "vp01")
+        w_grouped = [sb("wg%d" % h, [P, 2, P, 2], F32, "vp01", 2048 * h) for h in range(HALVES)]
         for h, engine in enumerate(("scalar", "vector")):
-            copy_out(engine, w_grouped[:, :, h], w_turned[h][:].rearrange("p c u q -> p c q u"))
-        turned3 = bank("turn3", [P, 1, 2, P], 0)
-        turn_values(RECENT, 3, turned3[:, 0])
-        pair = sb("vg_pair", [P, 2, P, 2], F32)
-        copy_turned("vector", pair[:], turned01)
-        warm = bank("warm", [P, Q + P], 4)
+            copy_out(engine, w_grouped[h][:], w_turned[h][:].rearrange("p c u q -> p c q u"))
+        warm = bank("warm", [P, Q + P], 0)
         for first, count in ((0, P), (P, Q)):
             nc.tensor.matmul_mx(out=warm[:, first:first + count], lhsT=q_codes[:, 0:P].bitcast(FP8X4),
                                 lhsT_scale=q_scales[:, 0:P], rhs=q_codes[:, 0:count].bitcast(FP8X4),
                                 rhs_scale=q_scales[:, 0:count], start=True, stop=True)
-        w_codes = sb("wc", [P, 2, Q], U32)
-        w_scales = sb("ws", [P, 2, Q], U8)
-        nc.vector.quantize_mx(out=w_codes[:].rearrange("p c q -> p (c q)").bitcast(FP8X4),
-                              scales=w_scales[:].rearrange("p c q -> p (c q)"),
-                              in_=w_grouped[:].rearrange("p c h q u -> p (c h q u)").bitcast(BF16))
-        grouped3 = sb("vg_recent3", [P, 1, P, 2], F32, "wg")
+        w_codes = [sb("wc%d" % h, [P, 2, P], U32) for h in range(HALVES)]
+        w_scales = [sb("ws%d" % h, [P, 2, P], U8) for h in range(HALVES)]
+        for h in range(HALVES):
+            nc.vector.quantize_mx(out=w_codes[h][:].rearrange("p c q -> p (c q)").bitcast(FP8X4),
+                                  scales=w_scales[h][:].rearrange("p c q -> p (c q)"),
+                                  in_=w_grouped[h][:].rearrange("p c q u -> p (c q u)").bitcast(BF16))
+        pair = sb("vg_pair", [P, 2, P, 2], F32, "wg0")
+        copy_turned("vector", pair[:], turned01)
+        turned3 = bank("turn3", [P, 1, 2, P], 2)
+        turn_values(RECENT, 3, turned3[:, 0])
+        grouped3 = sb("vg_recent3", [P, 1, P, 2], F32, "wg1")
         copy_turned("vector", grouped3[:], turned3)
         gather("scalar", LONG, 2)
 
@@ -262,15 +263,16 @@ def tile_attend_two_caches_pl_kernel(tc, query, keys_words, keys_scales, rkey_wo
         out_rows = out_0.rearrange("(p r) q -> p r q", r=PACK)
         halves = [slice(h * P, (h + 1) * P) for h in range(HALVES)]
 
-        def multiply(dst, c, r, start, stop, columns=slice(0, Q)):
+        def multiply(dst, c, r, h, start, stop):
             nc.tensor.matmul_mx(out=dst, lhsT=v_codes[c, r].bitcast(FP8X4), lhsT_scale=v_scales[c, r],
-                                rhs=w_codes[:, c, columns].bitcast(FP8X4), rhs_scale=w_scales[:, c, columns],
+                                rhs=w_codes[h][:, c].bitcast(FP8X4), rhs_scale=w_scales[h][:, c],
                                 start=start, stop=stop)
 
-        multiply(early[:, 0, :], RECENT, 0, True, False)
-        multiply(early[:, 1, :], RECENT, 1, False, False)
-        multiply(third[:], RECENT, 2, True, False)
-        turned2 = bank("turn2", [P, 1, 2, P], 0)
+        for h in range(HALVES):
+            multiply(early[:, 0, halves[h]], RECENT, 0, h, h == 0, False)
+            multiply(early[:, 1, halves[h]], RECENT, 1, h, False, False)
+            multiply(third[:, halves[h]], RECENT, 2, h, h == 0, False)
+        turned2 = bank("turn2", [P, 1, 2, P], 4)
         turn_values(LONG, 2, turned2[:, 0])
 
         gather("vector", LONG, 3, 0, SHARE)
@@ -280,15 +282,17 @@ def tile_attend_two_caches_pl_kernel(tc, query, keys_words, keys_scales, rkey_wo
         quantize_values("b", [(LONG, 0), (LONG, 1)], pair[:], "vp03", 1024)
         quantize_values("c", [(RECENT, 3)], grouped3[:], "vp03", 2048)
         one_part(LONG, 3, 7)
-        multiply(early[:, 0, :], LONG, 0, False, False)
-        multiply(early[:, 1, :], LONG, 1, False, True)
+        for r in range(2):
+            for h in range(HALVES):
+                multiply(early[:, r, halves[h]], LONG, r, h, False, r == 1 and h == 1)
         quantize_values("d", [(LONG, 2)], grouped2[:])
-        multiply(third[:], LONG, 2, False, True)
         for h in range(HALVES):
-            multiply(last[h][:], RECENT, 3, True, False, halves[h])
+            multiply(third[:, halves[h]], LONG, 2, h, False, h == 1)
+        for h in range(HALVES):
+            multiply(last[h][:], RECENT, 3, h, True, False)
         quantize_values("e", [(LONG, 3)], grouped[LONG, 3][:])
         for h in range(HALVES):
-            multiply(last[h][:], LONG, 3, False, True, halves[h])
+            multiply(last[h][:], LONG, 3, h, False, True)
 
         out_sb = sb("out_sb", [P, PACK, Q], F32)
         nc.scalar.copy(out=out_sb[:, 0:2, :], in_=early[:])

from contextlib import ExitStack

import concourse.mybir as mybir

F32 = mybir.dt.float32
BF16 = mybir.dt.bfloat16
I32 = mybir.dt.int32
U32 = mybir.dt.uint32
U16 = mybir.dt.uint16
U8 = mybir.dt.uint8
FP8X4 = mybir.dt.float8_e4m3fn_x4
FP4X4 = mybir.dt.float4_e2m1fn_x4
ACT = mybir.ActivationFunctionType
ALU = mybir.AluOpType

P = 128
PACK = 4
D, T, Q, E, U, SLOTS = 512, 2048, 256, 512, 1024, 512
HALVES = Q // P
FLOPS = 2 * 2 * D * Q * SLOTS + 2 * 2 * SLOTS * E * Q
BYTES_OF = {F32: 4, U32: 4, BF16: 2, U16: 2, U8: 1}
LONG, RECENT = 0, 1
SHARE = 288
ROUND_SHARE = 160


def tile_attend_two_caches_pl_kernel(tc, query, keys_words, keys_scales, rkey_words, rkey_scales,
                                         size, rsz, vals, rval, offs, offs2, out_0, out_1, out_2):
    nc = tc.nc
    with ExitStack() as ctx:
        keep = ctx.enter_context(tc.tile_pool(name="keep", bufs=1))
        work = ctx.enter_context(tc.tile_pool(name="work", bufs=1))
        psum = ctx.enter_context(tc.psum_pool(name="psum", bufs=1))
        place = {"free": 0}

        def sb(name, shape, dtype, on=None, skip=0):
            if on is None:
                nbytes = BYTES_OF[dtype]
                for n in shape[1:]:
                    nbytes = nbytes * n
                place[name] = place["free"]
                place["free"] = place["free"] + (nbytes + 63) // 64 * 64
            else:
                place[name] = place[on] + skip
            return work.tile(shape, dtype, name=name, align_bytes=64, offset=place[name])

        def bank(name, shape, number):
            return psum.tile(shape, F32, name=name, tag="bank%d" % number)

        scale_row = (0, 4)
        lists = [keep.tile([P, SLOTS // 16], U16, name="list0"), keep.tile([P, SLOTS // 16], U16, name="list1")]
        pools = (vals, rval)
        widths = (T, U)
        val_pool, key_scale_pool, key_word_pool = {}, {}, {}

        def load_scales(c, src):
            key_scale_pool[c] = sb("ksp%d" % c, [P, widths[c]], U8)
            nc.vector.memset(key_scale_pool[c][:].bitcast(I32), 0)
            rows = src[0].rearrange("(quad j) n -> j quad n", j=4)
            for j in range(4):
                nc.sync.dma_start(out=key_scale_pool[c][scale_row[c] + j:P:32, :].bitcast(I32), in_=rows[j].bitcast(I32))

        def load_values(c, r):
            val_pool[c, r] = sb("vp%d%d" % (c, r), [P, widths[c]], F32)
            nc.sync.dma_start(out=val_pool[c, r][:], in_=pools[c].rearrange("(m r) t -> r m t", r=PACK)[r])

        size_rows = sb("size_rows", [P, P], F32)

        def load_sizes(c):
            nc.sync.dma_start(out=size_rows[PACK * c:PACK * c + PACK, :],
                              in_=(size, rsz)[c].rearrange("o (j s) -> (o j) s", j=PACK))

        key_word_pool[RECENT] = sb("kwp1", [P, U], U32)
        nc.sync.dma_start(out=key_word_pool[RECENT][:].bitcast(I32),
                          in_=rkey_words[0].rearrange("p n t -> p (n t)").bitcast(I32))
        nc.sync.dma_start(lists[RECENT][:], offs2)
        load_scales(RECENT, rkey_scales)
        nc.vector.memset(size_rows[:], 0.0)

        ident = sb("ident", [P, P], F32)
        zeros = sb("zeros", [P, P], F32)
        nc.gpsimd.memset(zeros[:], 0.0)
        nc.gpsimd.affine_select(out=ident[:], in_=zeros[:], compare_op=ALU.not_equal, fill=1.0, base=0,
                                pattern=[[-1, P]], channel_multiplier=1)

        q_raw = sb("q_raw", [P, PACK, Q], F32)
        nc.sync.dma_start(out=q_raw[:], in_=query.rearrange("(p j) q -> p j q", j=PACK))
        load_values(RECENT, 0)
        nc.sync.dma_start(lists[LONG][:], offs)
        load_scales(LONG, keys_scales)
        key_word_pool[LONG] = sb("kwp0", [P, T], U16)
        nc.sync.dma_start(out=key_word_pool[LONG][:].bitcast(I32), in_=keys_words[0].bitcast(I32))
        load_values(RECENT, 1)
        load_sizes(LONG)
        load_sizes(RECENT)
        load_values(RECENT, 2)
        load_values(RECENT, 3)
        for r in range(PACK):
            load_values(LONG, r)

        key_scales = [sb("ks0", [P, SLOTS], U8), sb("ks1", [P, SLOTS], U8)]
        key_words = [sb("kw0", [P, SLOTS], U16), sb("kw1", [P, SLOTS], U32)]
        nc.vector.tensor_copy(key_words[RECENT][:], key_word_pool[RECENT][:].indirect(lists[RECENT][:]))
        nc.vector.tensor_copy(key_scales[RECENT][:], key_scale_pool[RECENT][:].indirect(lists[RECENT][:]))
        nc.vector.tensor_copy(key_scales[LONG][:], key_scale_pool[LONG][:].indirect(lists[LONG][:]))

        q_bf = sb("q_bf", [P, Q, PACK], BF16)
        nc.scalar.activation(out=q_bf[:].rearrange("p (c i) t -> p c t i", i=4),
                             in_=q_raw[:].rearrange("p t (c i) -> p c t i", i=4), func=ACT.Copy)
        q_codes = sb("q_codes", [P, Q], U32)
        q_scales = sb("q_scales", [P, Q], U8)
        nc.vector.quantize_mx(out=q_codes[:].bitcast(FP8X4), scales=q_scales[:],
                              in_=q_bf[:].rearrange("p q t -> p (q t)"))
        nc.vector.tensor_copy(key_words[LONG][:], key_word_pool[LONG][:].indirect(lists[LONG][:]))

        fmts = (FP4X4, FP8X4)
        scores = {}

        def score(c):
            for h in range(HALVES):
                scores[c, h] = bank("score%d%d" % (c, h), [P, SLOTS], 2 * (1 - c) + h)
                nc.tensor.matmul_mx(out=scores[c, h][:],
                                    lhsT=q_codes[:, h * P:(h + 1) * P].bitcast(FP8X4),
                                    lhsT_scale=q_scales[:, h * P:(h + 1) * P],
                                    rhs=key_words[c][:].bitcast(fmts[c]), rhs_scale=key_scales[c][scale_row[c]:P, :],
                                    start=True, stop=True)

        picked, grouped, v_codes, v_scales = {}, {}, {}, {}

        def gather(engine, c, r, first=0, count=SLOTS, on=None, skip=0):
            if first == 0:
                picked[c, r] = sb("picked%d%d" % (c, r), [P, SLOTS], BF16, on, skip)
            dst = picked[c, r][:].rearrange("p (u b k) -> p b u k", u=2, k=16)[:, first // 32:(first + count) // 32]
            src = val_pool[c, r][:].indirect(lists[c][:, first // 16:(first + count) // 16])
            if engine == "scalar":
                nc.scalar.activation(out=dst, in_=src, func=ACT.Copy)
            else:
                nc.vector.tensor_copy(dst, src)

        def turn_values(c, r, dst):
            words = picked[c, r][:].bitcast(F32)
            for u in range(2):
                nc.tensor.transpose(dst[:, u, :], words[:, u * P:(u + 1) * P], ident[:])

        def copy_out(engine, dst, src):
            if engine == "scalar":
                nc.scalar.copy(out=dst, in_=src)
            else:
                nc.vector.tensor_copy(out=dst, in_=src)

        def copy_turned(engine, dst, turned):
            copy_out(engine, dst, turned[:].rearrange("p k u m -> p k m u"))

        def quantize_values(name, parts, src, on=None, skip=0):
            n = len(parts)
            codes = sb("vc" + name, [P, n * P], U32, on, skip)
            scales = sb("vs" + name, [P, n * P], U8)
            nc.vector.quantize_mx(out=codes[:].bitcast(FP8X4), scales=scales[:],
                                  in_=src.rearrange("p k m u -> p (k m u)").bitcast(BF16))
            for k, cr in enumerate(parts):
                v_codes[cr] = codes[:, k * P:(k + 1) * P]
                v_scales[cr] = scales[:, k * P:(k + 1) * P]

        def one_part(c, r, number, copier="scalar", on=None):
            turned = bank("turn%d%d" % (c, r), [P, 1, 2, P], number)
            turn_values(c, r, turned[:, 0])
            grouped[c, r] = sb("vg%d%d" % (c, r), [P, 1, P, 2], F32, on)
            copy_turned(copier, grouped[c, r][:], turned)

        score(RECENT)
        gather("scalar", RECENT, 0)
        recent = sb("vg_recent", [P, 3, P, 2], F32)
        turned0 = bank("turn0", [P, 1, 2, P], 2)
        turn_values(RECENT, 0, turned0[:, 0])
        copy_turned("scalar", recent[:, 0:1], turned0)
        score(LONG)
        gather("scalar", RECENT, 1)
        size_turned = bank("size_turned", [P, P], 6)
        nc.tensor.transpose(size_turned[:], size_rows[:], ident[:])
        gather("scalar", RECENT, 2)
        size_cols = sb("size_cols", [P, 2 * PACK], F32, "vp12", 128)
        nc.scalar.copy(out=size_cols[:], in_=size_turned[:, 0:2 * PACK])
        turned12 = bank("turn12", [P, 2, 2, P], 7)
        turn_values(RECENT, 1, turned12[:, 0])
        turn_values(RECENT, 2, turned12[:, 1])

        neg_first = [sb("neg_first%d" % h, [P, 1], F32, "kwp0", 64 * h) for h in range(HALVES)]
        neg_max = sb("neg_max", [P, HALVES], F32)
        row_sum = [sb("row_sum%d" % h, [P, 1], F32, "vp12", 64 * h) for h in range(HALVES)]
        neg_scores = [sb("neg_scores%d" % h, [P, 2, SLOTS], F32) for h in range(HALVES)]
        probs = [sb("probs0", [P, 2, SLOTS], F32), sb("probs1", [P, 2, SLOTS], F32)]

        def negate(c, h, start, least):
            nc.vector.tensor_scalar(out=neg_scores[h][:, c, :].rearrange("q (u b k) -> q u b k", u=2, k=16),
                                    in0=scores[c, h][:].rearrange("q (b u k) -> q u b k", u=2, k=16),
                                    scalar1=-1.0, scalar2=start, op0=ALU.mult, op1=ALU.min, accum_out=least)

        for h in range(HALVES):
            negate(RECENT, h, None, neg_first[h][:])
        for h in range(HALVES):
            negate(LONG, h, neg_first[h][:], neg_max[:, h:h + 1])
            nc.scalar.activation(out=probs[h][:], in_=neg_scores[h][:], func=ACT.Exp,
                                 bias=neg_max[:, h:h + 1], scale=-1.0, accum_out=row_sum[h][:])
        spread = {}
        for c in (RECENT, LONG):
            spread[c] = bank("spread%d" % c, [P, 2, 16, 16], 4 + c)
            for j in range(PACK):
                nc.tensor.transpose(spread[c][:, :, 4 * j:4 * j + 4, :].rearrange("q u b k -> q b u k"),
                                    size_cols[:, PACK * c + j:PACK * c + j + 1].to_broadcast([P, P]), ident[:])

        copy_turned("vector", recent[:, 1:3], turned12)
        inv_sum = [sb("inv_sum%d" % h, [P, 1], F32) for h in range(HALVES)]
        nc.vector.reciprocal(out=inv_sum[0][:], in_=row_sum[0][:])
        quantize_values("a", [(RECENT, r) for r in range(3)], recent[:], "neg_scores0")

        w_turned = [bank("wturn%d" % h, [P, 2, 2, P], h) for h in range(HALVES)]

        def weigh(h, c, on=None, skip=0):
            weights = sb("weights%d%d" % (c, h), [P, SLOTS], BF16, on, skip)
            nc.vector.scalar_tensor_tensor(out=weights[:], in0=probs[h][:, c, :], scalar=inv_sum[h][:],
                                           in1=spread[c][:].rearrange("q u b k -> q (u b k)"),
                                           op0=ALU.mult, op1=ALU.mult)
            words = weights[:].bitcast(F32)
            for u in range(2):
                nc.tensor.transpose(w_turned[h][:, c, u, :], words[:, u * P:(u + 1) * P], ident[:])

        weigh(0, RECENT)
        nc.vector.reciprocal(out=inv_sum[1][:], in_=row_sum[1][:])
        weigh(0, LONG)
        weigh(1, RECENT)
        weigh(1, LONG)
        gather("vector", RECENT, 3, on="row_sum1")
        gather("scalar", LONG, 0)
        gather("scalar", LONG, 1)
        turned01 = bank("turn01", [P, 2, 2, P], 4)
        turn_values(LONG, 0, turned01[:, 0])
        turn_values(LONG, 1, turned01[:, 1])
        w_grouped = [sb("wg%d" % h, [P, 2, P, 2], F32, "vp01", 2048 * h) for h in range(HALVES)]
        for h, engine in enumerate(("scalar", "vector")):
            copy_out(engine, w_grouped[h][:], w_turned[h][:].rearrange("p c u q -> p c q u"))
        warm = bank("warm", [P, Q + P], 0)
        for first, count in ((0, P), (P, Q)):
            nc.tensor.matmul_mx(out=warm[:, first:first + count], lhsT=q_codes[:, 0:P].bitcast(FP8X4),
                                lhsT_scale=q_scales[:, 0:P], rhs=q_codes[:, 0:count].bitcast(FP8X4),
                                rhs_scale=q_scales[:, 0:count], start=True, stop=True)
        w_codes = [sb("wc%d" % h, [P, 2, P], U32) for h in range(HALVES)]
        w_scales = [sb("ws%d" % h, [P, 2, P], U8) for h in range(HALVES)]
        for h in range(HALVES):
            nc.vector.quantize_mx(out=w_codes[h][:].rearrange("p c q -> p (c q)").bitcast(FP8X4),
                                  scales=w_scales[h][:].rearrange("p c q -> p (c q)"),
                                  in_=w_grouped[h][:].rearrange("p c q u -> p (c q u)").bitcast(BF16))
        pair = sb("vg_pair", [P, 2, P, 2], F32, "wg0")
        copy_turned("vector", pair[:], turned01)
        turned3 = bank("turn3", [P, 1, 2, P], 2)
        turn_values(RECENT, 3, turned3[:, 0])
        grouped3 = sb("vg_recent3", [P, 1, P, 2], F32, "wg1")
        copy_turned("vector", grouped3[:], turned3)
        gather("scalar", LONG, 2)

        early = bank("early", [P, 2, Q], 3)
        third = bank("third", [P, Q], 5)
        last = [bank("last0", [P, P], 6), bank("last1", [P, P], 1)]
        out_rows = out_0.rearrange("(p r) q -> p r q", r=PACK)
        halves = [slice(h * P, (h + 1) * P) for h in range(HALVES)]

        def multiply(dst, c, r, h, start, stop):
            nc.tensor.matmul_mx(out=dst, lhsT=v_codes[c, r].bitcast(FP8X4), lhsT_scale=v_scales[c, r],
                                rhs=w_codes[h][:, c].bitcast(FP8X4), rhs_scale=w_scales[h][:, c],
                                start=start, stop=stop)

        for h in range(HALVES):
            multiply(early[:, 0, halves[h]], RECENT, 0, h, h == 0, False)
            multiply(early[:, 1, halves[h]], RECENT, 1, h, False, False)
            multiply(third[:, halves[h]], RECENT, 2, h, h == 0, False)
        turned2 = bank("turn2", [P, 1, 2, P], 4)
        turn_values(LONG, 2, turned2[:, 0])

        gather("vector", LONG, 3, 0, SHARE)
        gather("scalar", LONG, 3, SHARE, SLOTS - SHARE)
        grouped2 = sb("vg_third", [P, 1, P, 2], F32, "vp03")
        copy_turned("scalar", grouped2[:], turned2)
        quantize_values("b", [(LONG, 0), (LONG, 1)], pair[:], "vp03", 1024)
        quantize_values("c", [(RECENT, 3)], grouped3[:], "vp03", 2048)
        one_part(LONG, 3, 7)
        for r in range(2):
            for h in range(HALVES):
                multiply(early[:, r, halves[h]], LONG, r, h, False, r == 1 and h == 1)
        quantize_values("d", [(LONG, 2)], grouped2[:])
        for h in range(HALVES):
            multiply(third[:, halves[h]], LONG, 2, h, False, h == 1)
        for h in range(HALVES):
            multiply(last[h][:], RECENT, 3, h, True, False)
        quantize_values("e", [(LONG, 3)], grouped[LONG, 3][:])
        for h in range(HALVES):
            multiply(last[h][:], LONG, 3, h, False, True)

        out_sb = sb("out_sb", [P, PACK, Q], F32)
        nc.scalar.copy(out=out_sb[:, 0:2, :], in_=early[:])
        nc.sync.dma_start(out=out_rows[:, 0:2, :], in_=out_sb[:, 0:2, :])
        nc.vector.tensor_copy(out=out_sb[:, 2, :], in_=third[:])
        nc.vector.tensor_copy(out=out_sb[:, 3, 0:P], in_=last[0][:])
        nc.scalar.copy(out=out_sb[:, 3, P:Q], in_=last[1][:])
        nc.sync.dma_start(out=out_rows[:, 2:4, :], in_=out_sb[:, 2:4, :])

        o_codes = sb("o_codes", [P, Q], U32)
        o_scales = sb("o_scales", [P, Q], U8)
        o_bf = sb("o_bf", [P, Q, PACK], BF16)
        for engine, first, stop in (("vector", 0, P), ("scalar", ROUND_SHARE, Q), ("vector", P, ROUND_SHARE)):
            copy_out(engine, o_bf[:, first:stop, :].rearrange("p (c i) r -> p c r i", i=4),
                     out_sb[:, :, first:stop].rearrange("p r (c i) -> p c r i", i=4))
        out_words = out_1[0].rearrange("p c t -> p (c t)").bitcast(I32)
        for h in range(HALVES):
            nc.vector.quantize_mx(out=o_codes[:, halves[h]].bitcast(FP8X4), scales=o_scales[:, halves[h]],
                                  in_=o_bf[:, halves[h], :].rearrange("p q r -> p (q r)"))
            nc.sync.dma_start(out=out_words[:, halves[h]], in_=o_codes[:, halves[h]].bitcast(I32))
        for quad in range(4):
            queue = nc.sync if quad < 1 else nc.scalar
            queue.dma_start(out=out_2[0, 4 * quad:4 * quad + 4, :].bitcast(I32),
                            in_=o_scales[32 * quad:32 * quad + 4, :].bitcast(I32))
